import numpy as np
import ml_dtypes


def mxq(x, axis, fmt="e4m3"):
    dtype, down = {"e4m3": (ml_dtypes.float8_e4m3fn, 7), "e5m2": (ml_dtypes.float8_e5m2, 14)}[fmt]
    v = np.moveaxis(np.asarray(x, np.float32).astype(ml_dtypes.bfloat16).astype(np.float64), axis, -1)
    blocks = v.reshape(v.shape[:-1] + (-1, 32))
    amax = np.abs(blocks).max(-1, keepdims=True)
    byte = np.maximum(np.where(amax > 0, np.frexp(amax)[1] - 1 + 127, 0) - down, 1)
    scale = np.exp2(byte - 127.0)
    codes = (blocks / scale).astype(np.float32).astype(dtype).astype(np.float64)
    return np.moveaxis((codes * scale).reshape(v.shape), -1, axis)


WIDE = False


def mx_kscale(k):
    if not WIDE:
        return np.ones(k)
    levels = np.array([10, -10, 5, -5, 0])
    if k % 512:
        return np.exp2(np.random.permutation(np.resize(levels, k // 32))).repeat(32)
    a = np.empty((k // 512, 16))
    for p in range(k // 512):
        a[p, :8] = np.random.permutation(np.resize(levels, 8))
        for g in range(8):
            far = levels[np.abs(levels - a[p, g]) >= 10]
            a[p, g + 8] = far[np.random.randint(len(far))]
    return np.exp2(a.ravel()).repeat(32)


def f64(x):
    return np.asarray(x).astype(np.float64)


def striped(idx):
    return np.tile(idx.reshape(-1, 16).T, (8, 1)).astype(np.uint16)


def unstriped(offs):
    return offs[:16].T.reshape(-1).astype(np.int64)


def striped8(idx):
    return np.concatenate([x.reshape(-1, 16).T for x in idx]).astype(np.uint16)


def runs(offs, k):
    lists = np.stack([offs[16 * r : 16 * r + 16].T.reshape(-1) for r in range(8)]).astype(np.int64)
    return lists[np.arange(k) % 512 // 64]


def pack_weight(w):
    k, n = w.shape
    w = f64(np.asarray(w, np.float32).astype(ml_dtypes.bfloat16)).reshape(k // 32, 32, n)
    amax = np.abs(w).max(1)
    byte = np.clip(np.where(amax > 0, np.frexp(amax)[1] - 1 + 127 - 7, 1), 1, 254)
    scaled = (w * np.exp2(127.0 - byte)[:, None, :]).reshape(k, n).astype(np.float32)
    words = np.ascontiguousarray(scaled.reshape(k // 512, 128, 4, n).transpose(0, 1, 3, 2)).astype(ml_dtypes.float8_e4m3fn).view(np.uint8)
    return words, np.ascontiguousarray(byte.astype(np.uint8).reshape(k // 512, 16, n))


def unpack_weight(words, scales):
    g, p, n, _ = words.shape
    vals = np.ascontiguousarray(words).view(ml_dtypes.float8_e4m3fn).astype(np.float64) * np.repeat(np.exp2(scales.astype(np.float64) - 127.0), 8, axis=1)[..., None]
    return vals.transpose(0, 1, 3, 2).reshape(g * 512, n)


def relu(v):
    return np.maximum(v, 0.0)

def planes(y):
    n, m = y.shape
    v = y.astype(np.float32).astype(ml_dtypes.bfloat16).astype(np.float64).reshape(n // 32, 32, m)
    top = np.abs(v).max(1)
    byte = np.clip(np.where(top > 0, np.frexp(top)[1] - 1 + 127 - 7, 1), 1, 254)
    codes = (v * np.exp2(127.0 - byte)[:, None, :]).reshape(n, m).astype(np.float32).astype(ml_dtypes.float8_e4m3fn).view(np.uint8)
    words = codes.reshape(n // 512, 128, 4, m).transpose(0, 1, 3, 2)
    return np.ascontiguousarray(words), np.ascontiguousarray(byte.astype(np.uint8).reshape(n // 512, 16, m))


K, T, S, N, H, U = 1024, 2048, 512, 512, 512, 512


def setup_inputs():
    n = np.random.standard_normal
    s = mx_kscale(K)[:, None]
    u = mx_kscale(H)
    packed_xT = pack_weight(n((K, T)) * s)
    packed_w2 = pack_weight(n((H, N)) / np.sqrt(H) / u[:, None])
    return {
        "x_words": packed_xT[0],
        "x_scales": packed_xT[1],
        "w1": (n((K, H)) / np.sqrt(K) / s * u).astype(np.float32),
        "slope": np.random.uniform(-0.5, 0.5, (H, U)).astype(np.float32),
        "w2_words": packed_w2[0],
        "w2_scales": packed_w2[1],
        "offs": striped(np.random.permutation(T)[:S]),
        "task": striped8(np.stack([np.random.permutation(U)[(U * np.random.uniform(0, 1, S) ** 4).astype(np.int64)] for _ in range(8)])),
    }


def reference(x_words, x_scales, w1, slope, w2_words, w2_scales, offs, task):
    xq = unpack_weight(x_words, x_scales)[:, unstriped(offs)]
    y = mxq(f64(w1), 0, "e4m3").T @ xq
    q = relu(y)
    z = q + (y - q) * (f64(slope)[np.arange(H)[:, None], runs(task, H)])
    out_0 = unpack_weight(w2_words, w2_scales).T @ mxq(z, 0, "e4m3")
    return (out_0,) + planes(out_0)

@@ -1,0 +1,193 @@
+from contextlib import ExitStack
+
+import concourse.mybir as mybir
+
+K, T, S, H, N, U = 1024, 2048, 512, 512, 512, 512
+FLOPS = 2 * K * H * S + 2 * H * N * S
+
+F32 = mybir.dt.float32
+BF16 = mybir.dt.bfloat16
+I32 = mybir.dt.int32
+U32 = mybir.dt.uint32
+U16 = mybir.dt.uint16
+U8 = mybir.dt.uint8
+FP8X4 = mybir.dt.float8_e4m3fn_x4
+ALU = mybir.AluOpType
+ACT = mybir.ActivationFunctionType
+
+P = 128
+PACK = 4
+PASSES = K // (P * PACK)
+CH = 128
+NCH = S // CH
+HALF = S // 2
+
+
+def tile_picked_prelu8_none_po_kernel(
+    tc, x_words, x_scales, w1, slope, w2_words, w2_scales, offs, task, out_0, out_1, out_2
+):
+    nc = tc.nc
+    with ExitStack() as ctx:
+        keep = ctx.enter_context(tc.tile_pool(name="keep", bufs=1))
+        psum = ctx.enter_context(tc.psum_pool(name="psum", bufs=1))
+
+        task_sb = keep.tile([P, S // 16], U16, name="task_sb")
+        offs_sb = keep.tile([P, S // 16], U16, name="offs_sb")
+        slope_sb = [keep.tile([P, U], F32, name="slope%d" % t, align_bytes=64) for t in range(PACK)]
+        w1_raw = [keep.tile([P, PACK, H], F32, name="w1raw%d" % g, align_bytes=64) for g in range(PASSES)]
+        x_all = [keep.tile([P, T], U32, name="xall%d" % g, align_bytes=64) for g in range(PASSES)]
+        xs_all = keep.tile([P, T], U8, name="xs_all", align_bytes=64)
+        w2_raw = keep.tile([P, N], I32, name="w2_raw", align_bytes=64)
+        w2s_raw = keep.tile([P, N], U8, name="w2s_raw", align_bytes=64)
+
+        nc.vector.memset(xs_all[:].bitcast(I32), 0)
+        nc.vector.memset(w2s_raw[:].bitcast(I32), 0)
+
+        slope_rows = slope.rearrange("(p t) u -> p t u", t=PACK)
+        nc.sync.dma_start(task_sb[:], task)
+        nc.sync.dma_start(slope_sb[0][:], slope_rows[:, 0, :])
+        nc.sync.dma_start(offs_sb[:], offs)
+        nc.sync.dma_start(slope_sb[1][:], slope_rows[:, 1, :])
+        for q in range(4):
+            nc.sync.dma_start(
+                xs_all[32 * q : 32 * q + 4 * PASSES, :].bitcast(I32), x_scales[:, 4 * q : 4 * q + 4, :].bitcast(I32)
+            )
+        w1_rows = w1.rearrange("(g p j) c -> g p j c", p=P, j=PACK)
+        nc.sync.dma_start(w1_raw[0][:], w1_rows[0])
+        nc.sync.dma_start(slope_sb[2][:], slope_rows[:, 2, :])
+        nc.sync.dma_start(slope_sb[3][:], slope_rows[:, 3, :])
+        nc.sync.dma_start(w1_raw[1][:], w1_rows[1])
+        nc.sync.dma_start(x_all[0][:].bitcast(I32), x_words[0].rearrange("p n t -> p (n t)").bitcast(I32))
+        for q in range(4):
+            nc.sync.dma_start(
+                w2s_raw[32 * q : 32 * q + 4, :].bitcast(I32), w2_scales[0, 4 * q : 4 * q + 4, :].bitcast(I32)
+            )
+        nc.sync.dma_start(x_all[1][:].bitcast(I32), x_words[1].rearrange("p n t -> p (n t)").bitcast(I32))
+        nc.sync.dma_start(w2_raw[:], w2_words[0].rearrange("p n t -> p (n t)").bitcast(I32))
+
+        picked_slope = keep.tile([P, PACK, S], F32, name="picked_slope", align_bytes=64)
+        for t in range(PACK):
+            for h in range(2):
+                nc.vector.tensor_copy(
+                    picked_slope[:, t, HALF * h : HALF * (h + 1)],
+                    slope_sb[t][:].indirect(task_sb[:, HALF // 16 * h : HALF // 16 * (h + 1)]),
+                )
+
+        xs_picked = keep.tile([P, S], U8, name="xs_picked", align_bytes=64)
+        nc.vector.tensor_copy(xs_picked[:], xs_all[:].indirect(offs_sb[:]))
+
+        w1_codes = [keep.tile([P, H], U32, name="w1codes%d" % g, align_bytes=64) for g in range(PASSES)]
+        w1_scale = [keep.tile([P, H], U8, name="w1scale%d" % g, align_bytes=64) for g in range(PASSES)]
+        for g in range(PASSES):
+            w1_bf = keep.tile([P, H * PACK], BF16, name="w1bf%d" % g, align_bytes=64)
+            nc.scalar.activation(
+                w1_bf[:].rearrange("p (t m j) -> p m t j", t=PACK, j=PACK),
+                w1_raw[g][:].rearrange("p j (m t) -> p m t j", t=PACK),
+                ACT.Copy,
+            )
+            nc.vector.quantize_mx(out=w1_codes[g][:].bitcast(FP8X4), scales=w1_scale[g][:], in_=w1_bf[:])
+
+        x_picked = [keep.tile([P, S], U32, name="xpicked%d" % g, align_bytes=64) for g in range(PASSES)]
+        nc.vector.tensor_copy(x_picked[0][:], x_all[0][:].indirect(offs_sb[:]))
+        w2_scale = keep.tile([P, N], U8, name="w2_scale", align_bytes=64)
+        nc.vector.tensor_copy(
+            w2_scale[:].rearrange("p (t m) -> p m t", t=PACK), w2s_raw[:].rearrange("p (m t) -> p m t", t=PACK)
+        )
+        for h in range(2):
+            nc.vector.tensor_copy(
+                x_picked[1][:, HALF * h : HALF * (h + 1)],
+                x_all[1][:].indirect(offs_sb[:, HALF // 16 * h : HALF // 16 * (h + 1)]),
+            )
+        w2_codes = keep.tile([P, N], I32, name="w2_codes", align_bytes=64)
+        nc.vector.tensor_copy(
+            w2_codes[:].rearrange("p (t m) -> p m t", t=PACK), w2_raw[:].rearrange("p (m t) -> p m t", t=PACK)
+        )
+
+        out_codes = keep.tile([P, S], U32, name="out_codes", align_bytes=64)
+        out_scale = keep.tile([P, S], U8, name="out_scale", align_bytes=64)
+        out_rows = out_0.rearrange("(p t) s -> p t s", t=PACK)
+        words_out = out_1[0].rearrange("p n t -> p (n t)").bitcast(I32)
+
+        y = [psum.tile([P, PACK, CH], F32, name="y%d" % c) for c in range(NCH)]
+        acc = [psum.tile([P, PACK, CH], F32, name="acc%d" % c) for c in range(NCH)]
+        z_codes = [keep.tile([P, CH], U32, name="zcodes%d" % c, align_bytes=64) for c in range(NCH)]
+        z_scale = [keep.tile([P, CH], U8, name="zscale%d" % c, align_bytes=64) for c in range(NCH)]
+
+        def first_product(c):
+            cols = slice(CH * c, CH * (c + 1))
+            for t in range(PACK):
+                feats = slice(P * t, P * (t + 1))
+                for g in range(PASSES):
+                    nc.tensor.matmul_mx(
+                        out=y[c][:, t, :],
+                        lhsT=w1_codes[g][:, feats].bitcast(FP8X4),
+                        lhsT_scale=w1_scale[g][:, feats],
+                        rhs=x_picked[g][:, cols].bitcast(FP8X4),
+                        rhs_scale=xs_picked[4 * g : P, cols],
+                        start=(g == 0),
+                        stop=(g == PASSES - 1),
+                    )
+
+        above = [keep.tile([P, CH, PACK], BF16, name="above%d" % c, align_bytes=64) for c in range(NCH)]
+        below = [keep.tile([P, CH, PACK], BF16, name="below%d" % c, align_bytes=64) for c in range(NCH)]
+        z = [keep.tile([P, CH * PACK], BF16, name="z%d" % c, align_bytes=64) for c in range(NCH)]
+        res = [keep.tile([P, PACK, CH], F32, name="res%d" % c, align_bytes=64) for c in range(NCH)]
+        res_bf = [keep.tile([P, CH, PACK], BF16, name="resbf%d" % c, align_bytes=64) for c in range(NCH)]
+
+        def split_signs(c):
+            cols = slice(CH * c, CH * (c + 1))
+            y_woven = y[c][:].rearrange("p t n -> p n t")
+            nc.vector.scalar_tensor_tensor(
+                below[c][:], y_woven, 0.0, picked_slope[:, :, cols].rearrange("p t n -> p n t"), ALU.min, ALU.mult
+            )
+            nc.scalar.activation(above[c][:], y_woven, ACT.Relu)
+
+        def join_signs(c):
+            nc.vector.tensor_tensor(
+                z[c][:], above[c][:].rearrange("p n t -> p (n t)"), below[c][:].rearrange("p n t -> p (n t)"), ALU.add
+            )
+
+        def second_product(c):
+            nc.vector.quantize_mx(out=z_codes[c][:].bitcast(FP8X4), scales=z_scale[c][:], in_=z[c][:])
+            for t in range(PACK):
+                rows = slice(P * t, P * (t + 1))
+                nc.tensor.matmul_mx(
+                    out=acc[c][:, t, :],
+                    lhsT=w2_codes[:, rows].bitcast(FP8X4),
+                    lhsT_scale=w2_scale[:, rows],
+                    rhs=z_codes[c][:].bitcast(FP8X4),
+                    rhs_scale=z_scale[c][:],
+                    start=True,
+                    stop=True,
+                )
+
+        def hand_out(c):
+            cols = slice(CH * c, CH * (c + 1))
+            nc.scalar.copy(res[c][:], acc[c][:])
+            nc.sync.dma_start(out_rows[:, :, cols], res[c][:])
+            if c % 2 == 0:
+                nc.scalar.copy(res_bf[c][:], acc[c][:].rearrange("p t n -> p n t"))
+            else:
+                nc.vector.tensor_copy(res_bf[c][:], res[c][:].rearrange("p t n -> p n t"))
+
+        def planes(c):
+            cols = slice(CH * c, CH * (c + 1))
+            nc.vector.quantize_mx(
+                out=out_codes[:, cols].bitcast(FP8X4),
+                scales=out_scale[:, cols],
+                in_=res_bf[c][:].rearrange("p n t -> p (n t)"),
+            )
+            if c % 2 == 1:
+                pair = slice(CH * (c - 1), CH * (c + 1))
+                nc.sync.dma_start(words_out[:, pair], out_codes[:, pair].bitcast(I32))
+
+        for c in range(NCH):
+            first_product(c)
+        stages = [split_signs, join_signs, second_product, hand_out, planes]
+        for step in range(NCH + len(stages) - 1):
+            for depth, stage in enumerate(stages):
+                if 0 <= step - depth < NCH:
+                    stage(step - depth)
+        for q in range(4):
+            eng = nc.sync if q % 2 == 0 else nc.scalar
+            eng.dma_start(out_2[0, 4 * q : 4 * q + 4, :].bitcast(I32), out_scale[32 * q : 32 * q + 4, :].bitcast(I32))

@@ -34,9 +34,9 @@ def tile_picked_prelu8_none_po_kernel(
         task_sb = keep.tile([P, S // 16], U16, name="task_sb")
         offs_sb = keep.tile([P, S // 16], U16, name="offs_sb")
         slope_sb = [keep.tile([P, U], F32, name="slope%d" % t, align_bytes=64) for t in range(PACK)]
-        w1_raw = [keep.tile([P, PACK, H], F32, name="w1raw%d" % g, align_bytes=64) for g in range(PASSES)]
+        w1_raw = [keep.tile([P, PACK, H], F32, name="w1raw%d" % g, tag="w1raw%d" % g, align_bytes=64) for g in range(PASSES)]
         x_all = [keep.tile([P, T], U32, name="xall%d" % g, align_bytes=64) for g in range(PASSES)]
-        xs_all = keep.tile([P, T], U8, name="xs_all", align_bytes=64)
+        xs_all = keep.tile([P, T], U8, name="xs_all", tag="w1codes1", align_bytes=64)
         w2_raw = keep.tile([P, N], I32, name="w2_raw", align_bytes=64)
         w2s_raw = keep.tile([P, N], U8, name="w2s_raw", align_bytes=64)
 
@@ -44,19 +44,23 @@ def tile_picked_prelu8_none_po_kernel(
         nc.vector.memset(w2s_raw[:].bitcast(I32), 0)
 
         slope_rows = slope.rearrange("(p t) u -> p t u", t=PACK)
+        w1_rows = w1.rearrange("(g p j) c -> g p j c", p=P, j=PACK)
+
+        def load_x_scales(g):
+            for q in range(4):
+                nc.sync.dma_start(
+                    xs_all[32 * q + 4 * g : 32 * q + 4 * g + 4, :].bitcast(I32),
+                    x_scales[g, 4 * q : 4 * q + 4, :].bitcast(I32),
+                )
+
         nc.sync.dma_start(task_sb[:], task)
         nc.sync.dma_start(slope_sb[0][:], slope_rows[:, 0, :])
         nc.sync.dma_start(offs_sb[:], offs)
-        nc.sync.dma_start(slope_sb[1][:], slope_rows[:, 1, :])
-        for q in range(4):
-            nc.sync.dma_start(
-                xs_all[32 * q : 32 * q + 4 * PASSES, :].bitcast(I32), x_scales[:, 4 * q : 4 * q + 4, :].bitcast(I32)
-            )
-        w1_rows = w1.rearrange("(g p j) c -> g p j c", p=P, j=PACK)
-        nc.sync.dma_start(w1_raw[0][:], w1_rows[0])
-        nc.sync.dma_start(slope_sb[2][:], slope_rows[:, 2, :])
-        nc.sync.dma_start(slope_sb[3][:], slope_rows[:, 3, :])
-        nc.sync.dma_start(w1_raw[1][:], w1_rows[1])
+        for t in range(1, PACK):
+            nc.sync.dma_start(slope_sb[t][:], slope_rows[:, t, :])
+        for g in range(PASSES):
+            nc.sync.dma_start(w1_raw[g][:], w1_rows[g])
+            load_x_scales(g)
         nc.sync.dma_start(x_all[0][:].bitcast(I32), x_words[0].rearrange("p n t -> p (n t)").bitcast(I32))
         for q in range(4):
             nc.sync.dma_start(
@@ -76,7 +80,7 @@ def tile_picked_prelu8_none_po_kernel(
         xs_picked = keep.tile([P, S], U8, name="xs_picked", align_bytes=64)
         nc.vector.tensor_copy(xs_picked[:], xs_all[:].indirect(offs_sb[:]))
 
-        w1_codes = [keep.tile([P, H], U32, name="w1codes%d" % g, align_bytes=64) for g in range(PASSES)]
+        w1_codes = [keep.tile([P, H], U32, name="w1codes%d" % g, tag="w1codes%d" % g, align_bytes=64) for g in range(PASSES)]
         w1_scale = [keep.tile([P, H], U8, name="w1scale%d" % g, align_bytes=64) for g in range(PASSES)]
         for g in range(PASSES):
             w1_bf = keep.tile([P, H * PACK], BF16, name="w1bf%d" % g, align_bytes=64)
@@ -86,6 +90,14 @@ def tile_picked_prelu8_none_po_kernel(
                 ACT.Copy,
             )
             nc.vector.quantize_mx(out=w1_codes[g][:].bitcast(FP8X4), scales=w1_scale[g][:], in_=w1_bf[:])
+
+        woven_slope = keep.tile([P, S, PACK], F32, name="woven_slope", tag="w1raw%d" % (PASSES - 1), align_bytes=64)
+        for c in range(NCH):
+            cols = slice(CH * c, CH * (c + 1))
+            nc.scalar.copy(
+                woven_slope[:, cols, :].rearrange("p (c i) t -> p c t i", i=4),
+                picked_slope[:, :, cols].rearrange("p t (c i) -> p c t i", i=4),
+            )
 
         x_picked = [keep.tile([P, S], U32, name="xpicked%d" % g, align_bytes=64) for g in range(PASSES)]
         nc.vector.tensor_copy(x_picked[0][:], x_all[0][:].indirect(offs_sb[:]))
@@ -113,20 +125,18 @@ def tile_picked_prelu8_none_po_kernel(
         z_codes = [keep.tile([P, CH], U32, name="zcodes%d" % c, align_bytes=64) for c in range(NCH)]
         z_scale = [keep.tile([P, CH], U8, name="zscale%d" % c, align_bytes=64) for c in range(NCH)]
 
-        def first_product(c):
+        def first_product(c, t, g):
             cols = slice(CH * c, CH * (c + 1))
-            for t in range(PACK):
-                feats = slice(P * t, P * (t + 1))
-                for g in range(PASSES):
-                    nc.tensor.matmul_mx(
-                        out=y[c][:, t, :],
-                        lhsT=w1_codes[g][:, feats].bitcast(FP8X4),
-                        lhsT_scale=w1_scale[g][:, feats],
-                        rhs=x_picked[g][:, cols].bitcast(FP8X4),
-                        rhs_scale=xs_picked[4 * g : P, cols],
-                        start=(g == 0),
-                        stop=(g == PASSES - 1),
-                    )
+            feats = slice(P * t, P * (t + 1))
+            nc.tensor.matmul_mx(
+                out=y[c][:, t, :],
+                lhsT=w1_codes[g][:, feats].bitcast(FP8X4),
+                lhsT_scale=w1_scale[g][:, feats],
+                rhs=x_picked[g][:, cols].bitcast(FP8X4),
+                rhs_scale=xs_picked[4 * g : P, cols],
+                start=(g == 0),
+                stop=(g == PASSES - 1),
+            )
 
         above = [keep.tile([P, CH, PACK], BF16, name="above%d" % c, align_bytes=64) for c in range(NCH)]
         below = [keep.tile([P, CH, PACK], BF16, name="below%d" % c, align_bytes=64) for c in range(NCH)]
@@ -137,9 +147,7 @@ def tile_picked_prelu8_none_po_kernel(
         def split_signs(c):
             cols = slice(CH * c, CH * (c + 1))
             y_woven = y[c][:].rearrange("p t n -> p n t")
-            nc.vector.scalar_tensor_tensor(
-                below[c][:], y_woven, 0.0, picked_slope[:, :, cols].rearrange("p t n -> p n t"), ALU.min, ALU.mult
-            )
+            nc.vector.scalar_tensor_tensor(below[c][:], y_woven, 0.0, woven_slope[:, cols, :], ALU.min, ALU.mult)
             nc.scalar.activation(above[c][:], y_woven, ACT.Relu)
 
         def join_signs(c):
@@ -165,10 +173,10 @@ def tile_picked_prelu8_none_po_kernel(
             cols = slice(CH * c, CH * (c + 1))
             nc.scalar.copy(res[c][:], acc[c][:])
             nc.sync.dma_start(out_rows[:, :, cols], res[c][:])
-            if c % 2 == 0:
-                nc.scalar.copy(res_bf[c][:], acc[c][:].rearrange("p t n -> p n t"))
-            else:
-                nc.vector.tensor_copy(res_bf[c][:], res[c][:].rearrange("p t n -> p n t"))
+            nc.vector.tensor_copy(
+                res_bf[c][:].rearrange("p (c i) t -> p c t i", i=4),
+                res[c][:].rearrange("p t (c i) -> p c t i", i=4),
+            )
 
         def planes(c):
             cols = slice(CH * c, CH * (c + 1))
@@ -182,12 +190,18 @@ def tile_picked_prelu8_none_po_kernel(
                 nc.sync.dma_start(words_out[:, pair], out_codes[:, pair].bitcast(I32))
 
         for c in range(NCH):
-            first_product(c)
-        stages = [split_signs, join_signs, second_product, hand_out, planes]
-        for step in range(NCH + len(stages) - 1):
-            for depth, stage in enumerate(stages):
-                if 0 <= step - depth < NCH:
-                    stage(step - depth)
+            first_product(c, 0, 0)
+        for c in range(NCH):
+            for t in range(PACK):
+                for g in range(PASSES):
+                    if (t, g) != (0, 0):
+                        first_product(c, t, g)
+        for c in range(NCH):
+            split_signs(c)
+            join_signs(c)
+            second_product(c)
+            hand_out(c)
+            planes(c)
         for q in range(4):
             eng = nc.sync if q % 2 == 0 else nc.scalar
             eng.dma_start(out_2[0, 4 * q : 4 * q + 4, :].bitcast(I32), out_scale[32 * q : 32 * q + 4, :].bitcast(I32))

@@ -41,7 +41,7 @@ def tile_picked_prelu8_none_po_kernel(
         w2s_raw = keep.tile([P, N], U8, name="w2s_raw", align_bytes=64)
 
         nc.vector.memset(xs_all[:].bitcast(I32), 0)
-        nc.vector.memset(w2s_raw[:].bitcast(I32), 0)
+        nc.gpsimd.memset(w2s_raw[:].bitcast(I32), 0)
 
         slope_rows = slope.rearrange("(p t) u -> p t u", t=PACK)
         w1_rows = w1.rearrange("(g p j) c -> g p j c", p=P, j=PACK)
@@ -56,18 +56,20 @@ def tile_picked_prelu8_none_po_kernel(
         nc.sync.dma_start(task_sb[:], task)
         nc.sync.dma_start(slope_sb[0][:], slope_rows[:, 0, :])
         nc.sync.dma_start(offs_sb[:], offs)
-        for t in range(1, PACK):
-            nc.sync.dma_start(slope_sb[t][:], slope_rows[:, t, :])
+        nc.sync.dma_start(slope_sb[1][:], slope_rows[:, 1, :])
+        nc.sync.dma_start(w1_raw[0][:], w1_rows[0])
+        load_x_scales(0)
+        nc.sync.dma_start(slope_sb[2][:], slope_rows[:, 2, :])
+        nc.sync.dma_start(slope_sb[3][:], slope_rows[:, 3, :])
+        nc.sync.dma_start(w1_raw[1][:], w1_rows[1])
+        load_x_scales(1)
         for g in range(PASSES):
-            nc.sync.dma_start(w1_raw[g][:], w1_rows[g])
-            load_x_scales(g)
-        nc.sync.dma_start(x_all[0][:].bitcast(I32), x_words[0].rearrange("p n t -> p (n t)").bitcast(I32))
+            nc.sync.dma_start(x_all[g][:].bitcast(I32), x_words[g].rearrange("p n t -> p (n t)").bitcast(I32))
+        nc.sync.dma_start(w2_raw[:], w2_words[0].rearrange("p n t -> p (n t)").bitcast(I32))
         for q in range(4):
-            nc.sync.dma_start(
+            nc.gpsimd.dma_start(
                 w2s_raw[32 * q : 32 * q + 4, :].bitcast(I32), w2_scales[0, 4 * q : 4 * q + 4, :].bitcast(I32)
             )
-        nc.sync.dma_start(x_all[1][:].bitcast(I32), x_words[1].rearrange("p n t -> p (n t)").bitcast(I32))
-        nc.sync.dma_start(w2_raw[:], w2_words[0].rearrange("p n t -> p (n t)").bitcast(I32))
 
         picked_slope = keep.tile([P, PACK, S], F32, name="picked_slope", align_bytes=64)
         for t in range(PACK):
@@ -84,11 +86,12 @@ def tile_picked_prelu8_none_po_kernel(
         w1_scale = [keep.tile([P, H], U8, name="w1scale%d" % g, align_bytes=64) for g in range(PASSES)]
         for g in range(PASSES):
             w1_bf = keep.tile([P, H * PACK], BF16, name="w1bf%d" % g, align_bytes=64)
-            nc.scalar.activation(
-                w1_bf[:].rearrange("p (t m j) -> p m t j", t=PACK, j=PACK),
-                w1_raw[g][:].rearrange("p j (m t) -> p m t j", t=PACK),
-                ACT.Copy,
-            )
+            dealt = w1_bf[:].rearrange("p (t m j) -> p m t j", t=PACK, j=PACK)
+            raw = w1_raw[g][:].rearrange("p j (m t) -> p m t j", t=PACK)
+            on_scalar = P if g == 0 else P // 2
+            nc.scalar.activation(dealt[:, :on_scalar], raw[:, :on_scalar], ACT.Copy)
+            if on_scalar < P:
+                nc.vector.tensor_copy(dealt[:, on_scalar:], raw[:, on_scalar:])
             nc.vector.quantize_mx(out=w1_codes[g][:].bitcast(FP8X4), scales=w1_scale[g][:], in_=w1_bf[:])
 
         woven_slope = keep.tile([P, S, PACK], F32, name="woven_slope", tag="w1raw%d" % (PASSES - 1), align_bytes=64)
@@ -100,16 +103,16 @@ def tile_picked_prelu8_none_po_kernel(
             )
 
         x_picked = [keep.tile([P, S], U32, name="xpicked%d" % g, align_bytes=64) for g in range(PASSES)]
-        nc.vector.tensor_copy(x_picked[0][:], x_all[0][:].indirect(offs_sb[:]))
         w2_scale = keep.tile([P, N], U8, name="w2_scale", align_bytes=64)
-        nc.vector.tensor_copy(
-            w2_scale[:].rearrange("p (t m) -> p m t", t=PACK), w2s_raw[:].rearrange("p (m t) -> p m t", t=PACK)
+        nc.gpsimd.tensor_copy(
+            w2_scale[:].rearrange("p (t m) -> p t m", t=PACK), w2s_raw[:].rearrange("p (m t) -> p t m", t=PACK)
         )
-        for h in range(2):
-            nc.vector.tensor_copy(
-                x_picked[1][:, HALF * h : HALF * (h + 1)],
-                x_all[1][:].indirect(offs_sb[:, HALF // 16 * h : HALF // 16 * (h + 1)]),
-            )
+        for g in range(PASSES):
+            for h in range(2):
+                nc.vector.tensor_copy(
+                    x_picked[g][:, HALF * h : HALF * (h + 1)],
+                    x_all[g][:].indirect(offs_sb[:, HALF // 16 * h : HALF // 16 * (h + 1)]),
+                )
         w2_codes = keep.tile([P, N], I32, name="w2_codes", align_bytes=64)
         nc.vector.tensor_copy(
             w2_codes[:].rearrange("p (t m) -> p m t", t=PACK), w2_raw[:].rearrange("p (m t) -> p m t", t=PACK)

@@ -18,9 +18,14 @@ ACT = mybir.ActivationFunctionType
 P = 128
 PACK = 4
 PASSES = K // (P * PACK)
+QUADS = 4
+QUAD = P // QUADS
+ROWS = 4
+GROUP = 16
 CH = 128
 NCH = S // CH
 HALF = S // 2
+RUN = 4
 
 
 def tile_picked_prelu8_none_po_kernel(
@@ -31,12 +36,14 @@ def tile_picked_prelu8_none_po_kernel(
         keep = ctx.enter_context(tc.tile_pool(name="keep", bufs=1))
         psum = ctx.enter_context(tc.psum_pool(name="psum", bufs=1))
 
-        task_sb = keep.tile([P, S // 16], U16, name="task_sb")
-        offs_sb = keep.tile([P, S // 16], U16, name="offs_sb")
+        task_sb = keep.tile([P, S // GROUP], U16, name="task_sb")
+        offs_sb = keep.tile([P, S // GROUP], U16, name="offs_sb")
         slope_sb = [keep.tile([P, U], F32, name="slope%d" % t, align_bytes=64) for t in range(PACK)]
-        w1_raw = [keep.tile([P, PACK, H], F32, name="w1raw%d" % g, tag="w1raw%d" % g, align_bytes=64) for g in range(PASSES)]
+        w1_raw = [
+            keep.tile([P, PACK, H], F32, name="w1raw%d" % g, tag="w1raw%d" % g, align_bytes=64) for g in range(PASSES)
+        ]
         x_all = [keep.tile([P, T], U32, name="xall%d" % g, align_bytes=64) for g in range(PASSES)]
-        xs_all = keep.tile([P, T], U8, name="xs_all", tag="w1codes1", align_bytes=64)
+        xs_all = keep.tile([P, T], U8, name="xs_all", tag="w1codes%d" % (PASSES - 1), align_bytes=64)
         w2_raw = keep.tile([P, N], I32, name="w2_raw", align_bytes=64)
         w2s_raw = keep.tile([P, N], U8, name="w2s_raw", align_bytes=64)
 
@@ -46,12 +53,13 @@ def tile_picked_prelu8_none_po_kernel(
         slope_rows = slope.rearrange("(p t) u -> p t u", t=PACK)
         w1_rows = w1.rearrange("(g p j) c -> g p j c", p=P, j=PACK)
 
-        def load_x_scales(g):
-            for q in range(4):
-                nc.sync.dma_start(
-                    xs_all[32 * q + 4 * g : 32 * q + 4 * g + 4, :].bitcast(I32),
-                    x_scales[g, 4 * q : 4 * q + 4, :].bitcast(I32),
-                )
+        def load_x_scales(first):
+            for q in (first, first + 2):
+                for g in range(PASSES):
+                    nc.sync.dma_start(
+                        xs_all[QUAD * q + ROWS * g : QUAD * q + ROWS * (g + 1), :].bitcast(I32),
+                        x_scales[g, ROWS * q : ROWS * (q + 1), :].bitcast(I32),
+                    )
 
         nc.sync.dma_start(task_sb[:], task)
         nc.sync.dma_start(slope_sb[0][:], slope_rows[:, 0, :])
@@ -66,23 +74,28 @@ def tile_picked_prelu8_none_po_kernel(
         for g in range(PASSES):
             nc.sync.dma_start(x_all[g][:].bitcast(I32), x_words[g].rearrange("p n t -> p (n t)").bitcast(I32))
         nc.sync.dma_start(w2_raw[:], w2_words[0].rearrange("p n t -> p (n t)").bitcast(I32))
-        for q in range(4):
+        for q in range(QUADS):
             nc.gpsimd.dma_start(
-                w2s_raw[32 * q : 32 * q + 4, :].bitcast(I32), w2_scales[0, 4 * q : 4 * q + 4, :].bitcast(I32)
+                w2s_raw[QUAD * q : QUAD * q + ROWS, :].bitcast(I32),
+                w2_scales[0, ROWS * q : ROWS * (q + 1), :].bitcast(I32),
             )
+
+        def half_list(list_sb, h):
+            return list_sb[:, HALF // GROUP * h : HALF // GROUP * (h + 1)]
 
         picked_slope = keep.tile([P, PACK, S], F32, name="picked_slope", align_bytes=64)
         for t in range(PACK):
-            for h in range(2):
+            for h in range(S // HALF):
                 nc.vector.tensor_copy(
-                    picked_slope[:, t, HALF * h : HALF * (h + 1)],
-                    slope_sb[t][:].indirect(task_sb[:, HALF // 16 * h : HALF // 16 * (h + 1)]),
+                    picked_slope[:, t, HALF * h : HALF * (h + 1)], slope_sb[t][:].indirect(half_list(task_sb, h))
                 )
 
         xs_picked = keep.tile([P, S], U8, name="xs_picked", align_bytes=64)
         nc.vector.tensor_copy(xs_picked[:], xs_all[:].indirect(offs_sb[:]))
 
-        w1_codes = [keep.tile([P, H], U32, name="w1codes%d" % g, tag="w1codes%d" % g, align_bytes=64) for g in range(PASSES)]
+        w1_codes = [
+            keep.tile([P, H], U32, name="w1codes%d" % g, tag="w1codes%d" % g, align_bytes=64) for g in range(PASSES)
+        ]
         w1_scale = [keep.tile([P, H], U8, name="w1scale%d" % g, align_bytes=64) for g in range(PASSES)]
         for g in range(PASSES):
             w1_bf = keep.tile([P, H * PACK], BF16, name="w1bf%d" % g, align_bytes=64)
@@ -98,8 +111,8 @@ def tile_picked_prelu8_none_po_kernel(
         for c in range(NCH):
             cols = slice(CH * c, CH * (c + 1))
             nc.scalar.copy(
-                woven_slope[:, cols, :].rearrange("p (c i) t -> p c t i", i=4),
-                picked_slope[:, :, cols].rearrange("p t (c i) -> p c t i", i=4),
+                woven_slope[:, cols, :].rearrange("p (r i) t -> p r t i", i=RUN),
+                picked_slope[:, :, cols].rearrange("p t (r i) -> p r t i", i=RUN),
             )
 
         x_picked = [keep.tile([P, S], U32, name="xpicked%d" % g, align_bytes=64) for g in range(PASSES)]
@@ -108,10 +121,9 @@ def tile_picked_prelu8_none_po_kernel(
             w2_scale[:].rearrange("p (t m) -> p t m", t=PACK), w2s_raw[:].rearrange("p (m t) -> p t m", t=PACK)
         )
         for g in range(PASSES):
-            for h in range(2):
+            for h in range(S // HALF):
                 nc.vector.tensor_copy(
-                    x_picked[g][:, HALF * h : HALF * (h + 1)],
-                    x_all[g][:].indirect(offs_sb[:, HALF // 16 * h : HALF // 16 * (h + 1)]),
+                    x_picked[g][:, HALF * h : HALF * (h + 1)], x_all[g][:].indirect(half_list(offs_sb, h))
                 )
         w2_codes = keep.tile([P, N], I32, name="w2_codes", align_bytes=64)
         nc.vector.tensor_copy(
@@ -136,16 +148,19 @@ def tile_picked_prelu8_none_po_kernel(
                 lhsT=w1_codes[g][:, feats].bitcast(FP8X4),
                 lhsT_scale=w1_scale[g][:, feats],
                 rhs=x_picked[g][:, cols].bitcast(FP8X4),
-                rhs_scale=xs_picked[4 * g : P, cols],
+                rhs_scale=xs_picked[ROWS * g : P, cols],
                 start=(g == 0),
                 stop=(g == PASSES - 1),
             )
 
         above = [keep.tile([P, CH, PACK], BF16, name="above%d" % c, align_bytes=64) for c in range(NCH)]
         below = [keep.tile([P, CH, PACK], BF16, name="below%d" % c, align_bytes=64) for c in range(NCH)]
-        z = [keep.tile([P, CH * PACK], BF16, name="z%d" % c, align_bytes=64) for c in range(NCH)]
+        z = [keep.tile([P, CH * PACK], BF16, name="z%d" % c, tag="z%d" % c, align_bytes=64) for c in range(NCH)]
         res = [keep.tile([P, PACK, CH], F32, name="res%d" % c, align_bytes=64) for c in range(NCH)]
-        res_bf = [keep.tile([P, CH, PACK], BF16, name="resbf%d" % c, align_bytes=64) for c in range(NCH)]
+        res_bf = [
+            keep.tile([P, CH, PACK], BF16, name="resbf%d" % c, tag="z%d" % (NCH - 1 - c), align_bytes=64)
+            for c in range(NCH)
+        ]
 
         def split_signs(c):
             cols = slice(CH * c, CH * (c + 1))
@@ -161,11 +176,11 @@ def tile_picked_prelu8_none_po_kernel(
         def second_product(c):
             nc.vector.quantize_mx(out=z_codes[c][:].bitcast(FP8X4), scales=z_scale[c][:], in_=z[c][:])
             for t in range(PACK):
-                rows = slice(P * t, P * (t + 1))
+                dealt_cols = slice(P * t, P * (t + 1))
                 nc.tensor.matmul_mx(
                     out=acc[c][:, t, :],
-                    lhsT=w2_codes[:, rows].bitcast(FP8X4),
-                    lhsT_scale=w2_scale[:, rows],
+                    lhsT=w2_codes[:, dealt_cols].bitcast(FP8X4),
+                    lhsT_scale=w2_scale[:, dealt_cols],
                     rhs=z_codes[c][:].bitcast(FP8X4),
                     rhs_scale=z_scale[c][:],
                     start=True,
@@ -177,11 +192,11 @@ def tile_picked_prelu8_none_po_kernel(
             nc.scalar.copy(res[c][:], acc[c][:])
             nc.sync.dma_start(out_rows[:, :, cols], res[c][:])
             nc.vector.tensor_copy(
-                res_bf[c][:].rearrange("p (c i) t -> p c t i", i=4),
-                res[c][:].rearrange("p t (c i) -> p c t i", i=4),
+                res_bf[c][:].rearrange("p (r i) t -> p r t i", i=RUN),
+                res[c][:].rearrange("p t (r i) -> p r t i", i=RUN),
             )
 
-        def planes(c):
+        def quantize_out(c):
             cols = slice(CH * c, CH * (c + 1))
             nc.vector.quantize_mx(
                 out=out_codes[:, cols].bitcast(FP8X4),
@@ -203,8 +218,12 @@ def tile_picked_prelu8_none_po_kernel(
             split_signs(c)
             join_signs(c)
             second_product(c)
+        for c in range(NCH):
             hand_out(c)
-            planes(c)
-        for q in range(4):
-            eng = nc.sync if q % 2 == 0 else nc.scalar
-            eng.dma_start(out_2[0, 4 * q : 4 * q + 4, :].bitcast(I32), out_scale[32 * q : 32 * q + 4, :].bitcast(I32))
+            quantize_out(c)
+        for q in range(QUADS):
+            queue = nc.sync if q % 2 == 0 else nc.scalar
+            queue.dma_start(
+                out_2[0, ROWS * q : ROWS * (q + 1), :].bitcast(I32),
+                out_scale[QUAD * q : QUAD * q + ROWS, :].bitcast(I32),
+            )

@@ -149,8 +149,8 @@ def tile_picked_prelu8_none_po_kernel(
                 lhsT_scale=w1_scale[g][:, feats],
                 rhs=x_picked[g][:, cols].bitcast(FP8X4),
                 rhs_scale=xs_picked[ROWS * g : P, cols],
-                start=(g == 0),
-                stop=(g == PASSES - 1),
+                start=(g == 0 and t == 0),
+                stop=(g == PASSES - 1 and t == PACK - 1),
             )
 
         above = [keep.tile([P, CH, PACK], BF16, name="above%d" % c, align_bytes=64) for c in range(NCH)]
@@ -207,13 +207,10 @@ def tile_picked_prelu8_none_po_kernel(
                 pair = slice(CH * (c - 1), CH * (c + 1))
                 nc.sync.dma_start(words_out[:, pair], out_codes[:, pair].bitcast(I32))
 
-        for c in range(NCH):
-            first_product(c, 0, 0)
-        for c in range(NCH):
-            for t in range(PACK):
-                for g in range(PASSES):
-                    if (t, g) != (0, 0):
-                        first_product(c, t, g)
+        for g in range(PASSES):
+            for c in range(NCH):
+                for t in range(PACK):
+                    first_product(c, t, g)
         for c in range(NCH):
             split_signs(c)
             join_signs(c)

@@ -54,23 +54,23 @@ def tile_picked_prelu8_none_po_kernel(
         w1_rows = w1.rearrange("(g p j) c -> g p j c", p=P, j=PACK)
 
         def load_x_scales(first):
-            for q in (first, first + 2):
+            for r in (first, first + 1):
                 for g in range(PASSES):
                     nc.sync.dma_start(
-                        xs_all[QUAD * q + ROWS * g : QUAD * q + ROWS * (g + 1), :].bitcast(I32),
-                        x_scales[g, ROWS * q : ROWS * (q + 1), :].bitcast(I32),
+                        xs_all[ROWS * g + r : P : QUAD, :].bitcast(I32),
+                        x_scales[g].rearrange("(q r) n -> r q n", r=ROWS)[r].bitcast(I32),
                     )
 
-        nc.sync.dma_start(task_sb[:], task)
         nc.sync.dma_start(slope_sb[0][:], slope_rows[:, 0, :])
-        nc.sync.dma_start(offs_sb[:], offs)
+        nc.sync.dma_start(task_sb[:], task)
         nc.sync.dma_start(slope_sb[1][:], slope_rows[:, 1, :])
+        nc.sync.dma_start(offs_sb[:], offs)
         nc.sync.dma_start(w1_raw[0][:], w1_rows[0])
         load_x_scales(0)
         nc.sync.dma_start(slope_sb[2][:], slope_rows[:, 2, :])
         nc.sync.dma_start(slope_sb[3][:], slope_rows[:, 3, :])
         nc.sync.dma_start(w1_raw[1][:], w1_rows[1])
-        load_x_scales(1)
+        load_x_scales(2)
         for g in range(PASSES):
             nc.sync.dma_start(x_all[g][:].bitcast(I32), x_words[g].rearrange("p n t -> p (n t)").bitcast(I32))
         nc.sync.dma_start(w2_raw[:], w2_words[0].rearrange("p n t -> p (n t)").bitcast(I32))
@@ -127,7 +127,8 @@ def tile_picked_prelu8_none_po_kernel(
                 )
         w2_codes = keep.tile([P, N], I32, name="w2_codes", align_bytes=64)
         nc.vector.tensor_copy(
-            w2_codes[:].rearrange("p (t m) -> p m t", t=PACK), w2_raw[:].rearrange("p (m t) -> p m t", t=PACK)
+            w2_codes[:].rearrange("p (t r i) -> p r t i", t=PACK, i=RUN),
+            w2_raw[:].rearrange("p (r i t) -> p r t i", t=PACK, i=RUN),
         )
 
         out_codes = keep.tile([P, S], U32, name="out_codes", align_bytes=64)
@@ -218,9 +219,9 @@ def tile_picked_prelu8_none_po_kernel(
         for c in range(NCH):
             hand_out(c)
             quantize_out(c)
-        for q in range(QUADS):
-            queue = nc.sync if q % 2 == 0 else nc.scalar
+        for r in range(ROWS):
+            queue = nc.sync if r % 2 == 0 else nc.scalar
             queue.dma_start(
-                out_2[0, ROWS * q : ROWS * (q + 1), :].bitcast(I32),
-                out_scale[QUAD * q : QUAD * q + ROWS, :].bitcast(I32),
+                out_2[0].rearrange("(q r) n -> r q n", r=ROWS)[r].bitcast(I32),
+                out_scale[r:P:QUAD, :].bitcast(I32),
             )

@@ -21,6 +21,8 @@ PASSES = K // (P * PACK)
 QUADS = 4
 QUAD = P // QUADS
 ROWS = 4
+SPREAD = QUAD // ROWS
+PLANE = 4
 GROUP = 16
 CH = 128
 NCH = S // CH
@@ -38,42 +40,36 @@ def tile_picked_prelu8_none_po_kernel(
 
         task_sb = keep.tile([P, S // GROUP], U16, name="task_sb")
         offs_sb = keep.tile([P, S // GROUP], U16, name="offs_sb")
-        slope_sb = [keep.tile([P, U], F32, name="slope%d" % t, align_bytes=64) for t in range(PACK)]
+        slope_sb = [keep.tile([P, U], F32, name="slope%d" % t, tag="slope%d" % t, align_bytes=64) for t in range(PACK)]
         w1_raw = [
             keep.tile([P, PACK, H], F32, name="w1raw%d" % g, tag="w1raw%d" % g, align_bytes=64) for g in range(PASSES)
         ]
-        x_all = [keep.tile([P, T], U32, name="xall%d" % g, align_bytes=64) for g in range(PASSES)]
-        xs_all = keep.tile([P, T], U8, name="xs_all", tag="w1codes%d" % (PASSES - 1), align_bytes=64)
-        w2_raw = keep.tile([P, N], I32, name="w2_raw", align_bytes=64)
+        xs_all = keep.tile([P, PASSES, T], U8, name="xs_all", tag="xs_all", align_bytes=64)
+        xs_spread = keep.tile([P, PASSES * S], U8, name="xs_spread", align_bytes=64)
+        xs_picked = keep.tile([P, PASSES * S], U8, name="xs_picked", align_bytes=64)
         w2s_raw = keep.tile([P, N], U8, name="w2s_raw", align_bytes=64)
 
-        nc.vector.memset(xs_all[:].bitcast(I32), 0)
+        nc.vector.memset(xs_all[:].rearrange("p g n -> p (g n)").bitcast(I32), 0)
+        nc.vector.memset(xs_picked[:].bitcast(I32), 0)
         nc.gpsimd.memset(w2s_raw[:].bitcast(I32), 0)
 
         slope_rows = slope.rearrange("(p t) u -> p t u", t=PACK)
         w1_rows = w1.rearrange("(g p j) c -> g p j c", p=P, j=PACK)
 
-        def load_x_scales(first):
-            for r in (first, first + 1):
-                for g in range(PASSES):
-                    nc.sync.dma_start(
-                        xs_all[ROWS * g + r : P : QUAD, :].bitcast(I32),
-                        x_scales[g].rearrange("(q r) n -> r q n", r=ROWS)[r].bitcast(I32),
-                    )
-
         nc.sync.dma_start(slope_sb[0][:], slope_rows[:, 0, :])
         nc.sync.dma_start(task_sb[:], task)
         nc.sync.dma_start(slope_sb[1][:], slope_rows[:, 1, :])
         nc.sync.dma_start(offs_sb[:], offs)
+        nc.sync.dma_start(
+            xs_all[0:P:SPREAD, :, :].bitcast(I32), x_scales.rearrange("g b n -> b g n").bitcast(I32)
+        )
         nc.sync.dma_start(w1_raw[0][:], w1_rows[0])
-        load_x_scales(0)
         nc.sync.dma_start(slope_sb[2][:], slope_rows[:, 2, :])
-        nc.sync.dma_start(slope_sb[3][:], slope_rows[:, 3, :])
         nc.sync.dma_start(w1_raw[1][:], w1_rows[1])
-        load_x_scales(2)
-        for g in range(PASSES):
-            nc.sync.dma_start(x_all[g][:].bitcast(I32), x_words[g].rearrange("p n t -> p (n t)").bitcast(I32))
-        nc.sync.dma_start(w2_raw[:], w2_words[0].rearrange("p n t -> p (n t)").bitcast(I32))
+        nc.sync.dma_start(slope_sb[3][:], slope_rows[:, 3, :])
+        x_rows = [x_words[g].rearrange("p n t -> p (n t)").bitcast(I32) for g in range(PASSES)]
+        x_first = keep.tile([P, T], U32, name="x_first", align_bytes=64)
+        nc.sync.dma_start(x_first[:].bitcast(I32), x_rows[0])
         for q in range(QUADS):
             nc.gpsimd.dma_start(
                 w2s_raw[QUAD * q : QUAD * q + ROWS, :].bitcast(I32),
@@ -84,14 +80,27 @@ def tile_picked_prelu8_none_po_kernel(
             return list_sb[:, HALF // GROUP * h : HALF // GROUP * (h + 1)]
 
         picked_slope = keep.tile([P, PACK, S], F32, name="picked_slope", align_bytes=64)
-        for t in range(PACK):
+
+        def pick_slopes(t):
             for h in range(S // HALF):
                 nc.vector.tensor_copy(
                     picked_slope[:, t, HALF * h : HALF * (h + 1)], slope_sb[t][:].indirect(half_list(task_sb, h))
                 )
 
-        xs_picked = keep.tile([P, S], U8, name="xs_picked", align_bytes=64)
-        nc.vector.tensor_copy(xs_picked[:], xs_all[:].indirect(offs_sb[:]))
+        pick_slopes(0)
+        for g in range(PASSES):
+            nc.vector.tensor_copy(xs_spread[:, S * g : S * (g + 1)], xs_all[:, g, :].indirect(offs_sb[:]))
+        for r in range(ROWS):
+            nc.sync.dma_start(
+                xs_picked[PLANE + r : P : QUAD, :].bitcast(I32), xs_spread[SPREAD * r : P : QUAD, :].bitcast(I32)
+            )
+        x_last = keep.tile([P, T], U32, name="x_last", tag="xs_all", align_bytes=64)
+        nc.sync.dma_start(x_last[:].bitcast(I32), x_rows[1])
+        x_all = [x_first, x_last]
+        for t in range(1, PACK):
+            pick_slopes(t)
+        w2_raw = keep.tile([P, N], I32, name="w2_raw", tag="slope%d" % (PACK - 1), align_bytes=64)
+        nc.sync.dma_start(w2_raw[:], w2_words[0].rearrange("p n t -> p (n t)").bitcast(I32))
 
         w1_codes = [
             keep.tile([P, H], U32, name="w1codes%d" % g, tag="w1codes%d" % g, align_bytes=64) for g in range(PASSES)
@@ -101,7 +110,7 @@ def tile_picked_prelu8_none_po_kernel(
             w1_bf = keep.tile([P, H * PACK], BF16, name="w1bf%d" % g, align_bytes=64)
             dealt = w1_bf[:].rearrange("p (t m j) -> p m t j", t=PACK, j=PACK)
             raw = w1_raw[g][:].rearrange("p j (m t) -> p m t j", t=PACK)
-            on_scalar = P if g == 0 else P // 2
+            on_scalar = P if g == 0 else 3 * P // 4
             nc.scalar.activation(dealt[:, :on_scalar], raw[:, :on_scalar], ACT.Copy)
             if on_scalar < P:
                 nc.vector.tensor_copy(dealt[:, on_scalar:], raw[:, on_scalar:])
@@ -125,19 +134,13 @@ def tile_picked_prelu8_none_po_kernel(
                 nc.vector.tensor_copy(
                     x_picked[g][:, HALF * h : HALF * (h + 1)], x_all[g][:].indirect(half_list(offs_sb, h))
                 )
-        w2_codes = keep.tile([P, N], I32, name="w2_codes", align_bytes=64)
-        nc.vector.tensor_copy(
-            w2_codes[:].rearrange("p (t r i) -> p r t i", t=PACK, i=RUN),
-            w2_raw[:].rearrange("p (r i t) -> p r t i", t=PACK, i=RUN),
-        )
 
         out_codes = keep.tile([P, S], U32, name="out_codes", align_bytes=64)
         out_scale = keep.tile([P, S], U8, name="out_scale", align_bytes=64)
         out_rows = out_0.rearrange("(p t) s -> p t s", t=PACK)
         words_out = out_1[0].rearrange("p n t -> p (n t)").bitcast(I32)
 
-        y = [psum.tile([P, PACK, CH], F32, name="y%d" % c) for c in range(NCH)]
-        acc = [psum.tile([P, PACK, CH], F32, name="acc%d" % c) for c in range(NCH)]
+        y = [psum.tile([P, PACK, CH], F32, name="y%d" % c, tag="y%d" % c) for c in range(NCH)]
         z_codes = [keep.tile([P, CH], U32, name="zcodes%d" % c, align_bytes=64) for c in range(NCH)]
         z_scale = [keep.tile([P, CH], U8, name="zscale%d" % c, align_bytes=64) for c in range(NCH)]
 
@@ -149,25 +152,29 @@ def tile_picked_prelu8_none_po_kernel(
                 lhsT=w1_codes[g][:, feats].bitcast(FP8X4),
                 lhsT_scale=w1_scale[g][:, feats],
                 rhs=x_picked[g][:, cols].bitcast(FP8X4),
-                rhs_scale=xs_picked[ROWS * g : P, cols],
+                rhs_scale=xs_picked[PLANE:P, S * g + CH * c : S * g + CH * (c + 1)],
                 start=(g == 0 and t == 0),
                 stop=(g == PASSES - 1 and t == PACK - 1),
             )
 
-        above = [keep.tile([P, CH, PACK], BF16, name="above%d" % c, align_bytes=64) for c in range(NCH)]
-        below = [keep.tile([P, CH, PACK], BF16, name="below%d" % c, align_bytes=64) for c in range(NCH)]
+        above = [keep.tile([P, CH, PACK], BF16, name="above%d" % c, tag="above%d" % c, align_bytes=64) for c in range(NCH)]
+        below = [keep.tile([P, CH, PACK], BF16, name="below%d" % c, tag="below%d" % c, align_bytes=64) for c in range(NCH)]
         z = [keep.tile([P, CH * PACK], BF16, name="z%d" % c, tag="z%d" % c, align_bytes=64) for c in range(NCH)]
         res = [keep.tile([P, PACK, CH], F32, name="res%d" % c, align_bytes=64) for c in range(NCH)]
+        w2_codes = keep.tile([P, N], I32, name="w2_codes", align_bytes=64)
+        LAST = NCH - 1
+        res_tags = ["resbf0", "z%d" % LAST, "z%d" % (LAST - 1), "z%d" % (LAST - 2)]
         res_bf = [
-            keep.tile([P, CH, PACK], BF16, name="resbf%d" % c, tag="z%d" % (NCH - 1 - c), align_bytes=64)
-            for c in range(NCH)
+            keep.tile([P, CH, PACK], BF16, name="resbf%d" % c, tag=res_tags[c], align_bytes=64) for c in range(NCH)
         ]
 
-        def split_signs(c):
+        def keep_above(c):
+            nc.scalar.activation(above[c][:], y[c][:].rearrange("p t n -> p n t"), ACT.Relu)
+
+        def scale_below(c):
             cols = slice(CH * c, CH * (c + 1))
             y_woven = y[c][:].rearrange("p t n -> p n t")
             nc.vector.scalar_tensor_tensor(below[c][:], y_woven, 0.0, woven_slope[:, cols, :], ALU.min, ALU.mult)
-            nc.scalar.activation(above[c][:], y_woven, ACT.Relu)
 
         def join_signs(c):
             nc.vector.tensor_tensor(
@@ -175,24 +182,33 @@ def tile_picked_prelu8_none_po_kernel(
             )
 
         def second_product(c):
-            nc.vector.quantize_mx(out=z_codes[c][:].bitcast(FP8X4), scales=z_scale[c][:], in_=z[c][:])
-            for t in range(PACK):
-                dealt_cols = slice(P * t, P * (t + 1))
-                nc.tensor.matmul_mx(
-                    out=acc[c][:, t, :],
-                    lhsT=w2_codes[:, dealt_cols].bitcast(FP8X4),
-                    lhsT_scale=w2_scale[:, dealt_cols],
-                    rhs=z_codes[c][:].bitcast(FP8X4),
-                    rhs_scale=z_scale[c][:],
-                    start=True,
-                    stop=True,
-                )
-
-        def hand_out(c):
             cols = slice(CH * c, CH * (c + 1))
-            nc.scalar.copy(res[c][:], acc[c][:])
+            nc.vector.quantize_mx(out=z_codes[c][:].bitcast(FP8X4), scales=z_scale[c][:], in_=z[c][:])
+            parts = 2 if c == LAST else 1
+            width = PACK // parts
+            for part in range(parts):
+                tag = "acc%d" % c if part == 0 else "y0"
+                acc = psum.tile([P, width, CH], F32, name="acc%d_%d" % (c, part), tag=tag)
+                for i in range(width):
+                    dealt_cols = slice(P * (width * part + i), P * (width * part + i + 1))
+                    nc.tensor.matmul_mx(
+                        out=acc[:, i, :],
+                        lhsT=w2_codes[:, dealt_cols].bitcast(FP8X4),
+                        lhsT_scale=w2_scale[:, dealt_cols],
+                        rhs=z_codes[c][:].bitcast(FP8X4),
+                        rhs_scale=z_scale[c][:],
+                        start=True,
+                        stop=True,
+                    )
+                if part == 0:
+                    nc.scalar.copy(res[c][:, :width, :], acc[:])
+                else:
+                    nc.vector.tensor_copy(res[c][:, width:, :], acc[:])
             nc.sync.dma_start(out_rows[:, :, cols], res[c][:])
-            nc.vector.tensor_copy(
+
+        def round_out(c):
+            weave = nc.scalar.copy if c == 0 else nc.vector.tensor_copy
+            weave(
                 res_bf[c][:].rearrange("p (r i) t -> p r t i", i=RUN),
                 res[c][:].rearrange("p t (r i) -> p r t i", i=RUN),
             )
@@ -212,12 +228,28 @@ def tile_picked_prelu8_none_po_kernel(
             for c in range(NCH):
                 for t in range(PACK):
                     first_product(c, t, g)
+        nc.vector.tensor_copy(
+            w2_codes[:].rearrange("p (t r i) -> p r t i", t=PACK, i=RUN),
+            w2_raw[:].rearrange("p (r i t) -> p r t i", t=PACK, i=RUN),
+        )
         for c in range(NCH):
-            split_signs(c)
-            join_signs(c)
+            if c == 0:
+                scale_below(c)
+                nc.vector.scalar_tensor_tensor(
+                    z[c][:].rearrange("p (n t) -> p n t", t=PACK),
+                    y[c][:].rearrange("p t n -> p n t"),
+                    0.0,
+                    below[c][:],
+                    ALU.max,
+                    ALU.add,
+                )
+            else:
+                keep_above(c)
+                scale_below(c)
+                join_signs(c)
             second_product(c)
         for c in range(NCH):
-            hand_out(c)
+            round_out(c)
             quantize_out(c)
         for r in range(ROWS):
             queue = nc.sync if r % 2 == 0 else nc.scalar

@@ -51,7 +51,7 @@ def tile_picked_prelu8_none_po_kernel(
 
         nc.vector.memset(xs_all[:].rearrange("p g n -> p (g n)").bitcast(I32), 0)
         nc.vector.memset(xs_picked[:].bitcast(I32), 0)
-        nc.gpsimd.memset(w2s_raw[:].bitcast(I32), 0)
+        nc.vector.memset(w2s_raw[:].bitcast(I32), 0)
 
         slope_rows = slope.rearrange("(p t) u -> p t u", t=PACK)
         w1_rows = w1.rearrange("(g p j) c -> g p j c", p=P, j=PACK)
@@ -64,17 +64,16 @@ def tile_picked_prelu8_none_po_kernel(
             xs_all[0:P:SPREAD, :, :].bitcast(I32), x_scales.rearrange("g b n -> b g n").bitcast(I32)
         )
         nc.sync.dma_start(w1_raw[0][:], w1_rows[0])
+        for r in range(ROWS):
+            nc.sync.dma_start(
+                w2s_raw[r:P:QUAD, :].bitcast(I32), w2_scales[0].rearrange("(q r) n -> r q n", r=ROWS)[r].bitcast(I32)
+            )
         nc.sync.dma_start(slope_sb[2][:], slope_rows[:, 2, :])
         nc.sync.dma_start(w1_raw[1][:], w1_rows[1])
         nc.sync.dma_start(slope_sb[3][:], slope_rows[:, 3, :])
         x_rows = [x_words[g].rearrange("p n t -> p (n t)").bitcast(I32) for g in range(PASSES)]
-        x_first = keep.tile([P, T], U32, name="x_first", align_bytes=64)
+        x_first = keep.tile([P, T], U32, name="x_first", tag="x_first", align_bytes=64)
         nc.sync.dma_start(x_first[:].bitcast(I32), x_rows[0])
-        for q in range(QUADS):
-            nc.gpsimd.dma_start(
-                w2s_raw[QUAD * q : QUAD * q + ROWS, :].bitcast(I32),
-                w2_scales[0, ROWS * q : ROWS * (q + 1), :].bitcast(I32),
-            )
 
         def half_list(list_sb, h):
             return list_sb[:, HALF // GROUP * h : HALF // GROUP * (h + 1)]
@@ -125,15 +124,16 @@ def tile_picked_prelu8_none_po_kernel(
             )
 
         x_picked = [keep.tile([P, S], U32, name="xpicked%d" % g, align_bytes=64) for g in range(PASSES)]
-        w2_scale = keep.tile([P, N], U8, name="w2_scale", align_bytes=64)
-        nc.gpsimd.tensor_copy(
-            w2_scale[:].rearrange("p (t m) -> p t m", t=PACK), w2s_raw[:].rearrange("p (m t) -> p t m", t=PACK)
-        )
         for g in range(PASSES):
             for h in range(S // HALF):
                 nc.vector.tensor_copy(
                     x_picked[g][:, HALF * h : HALF * (h + 1)], x_all[g][:].indirect(half_list(offs_sb, h))
                 )
+
+        w2_scale = keep.tile([P, N], U8, name="w2_scale", tag="x_first", align_bytes=64)
+        nc.vector.tensor_copy(
+            w2_scale[:].rearrange("p (t m) -> p t m", t=PACK), w2s_raw[:].rearrange("p (m t) -> p t m", t=PACK)
+        )
 
         out_codes = keep.tile([P, S], U32, name="out_codes", align_bytes=64)
         out_scale = keep.tile([P, S], U8, name="out_scale", align_bytes=64)

@@ -28,6 +28,9 @@ CH = 128
 NCH = S // CH
 HALF = S // 2
 RUN = 4
+XSTEP = 4
+RES_TAGS = ["z2", "z3", "resbf2", "resbf3"]
+ROUND_ON_SCALAR = (2,)
 
 
 def tile_picked_prelu8_none_po_kernel(
@@ -38,47 +41,40 @@ def tile_picked_prelu8_none_po_kernel(
         keep = ctx.enter_context(tc.tile_pool(name="keep", bufs=1))
         psum = ctx.enter_context(tc.psum_pool(name="psum", bufs=1))
 
+        def sbuf(shape, dtype, name, takes_over=None):
+            return keep.tile(shape, dtype, name=name, tag=takes_over or name, align_bytes=64)
+
         task_sb = keep.tile([P, S // GROUP], U16, name="task_sb")
         offs_sb = keep.tile([P, S // GROUP], U16, name="offs_sb")
-        slope_sb = [keep.tile([P, U], F32, name="slope%d" % t, tag="slope%d" % t, align_bytes=64) for t in range(PACK)]
-        w1_raw = [
-            keep.tile([P, PACK, H], F32, name="w1raw%d" % g, tag="w1raw%d" % g, align_bytes=64) for g in range(PASSES)
-        ]
-        xs_all = keep.tile([P, PASSES, T], U8, name="xs_all", tag="xs_all", align_bytes=64)
-        xs_spread = keep.tile([P, PASSES * S], U8, name="xs_spread", align_bytes=64)
-        xs_picked = keep.tile([P, PASSES * S], U8, name="xs_picked", align_bytes=64)
-        w2s_raw = keep.tile([P, N], U8, name="w2s_raw", align_bytes=64)
-
-        nc.vector.memset(xs_all[:].rearrange("p g n -> p (g n)").bitcast(I32), 0)
-        nc.vector.memset(xs_picked[:].bitcast(I32), 0)
-        nc.vector.memset(w2s_raw[:].bitcast(I32), 0)
-
         slope_rows = slope.rearrange("(p t) u -> p t u", t=PACK)
         w1_rows = w1.rearrange("(g p j) c -> g p j c", p=P, j=PACK)
+        x_rows = [x_words[g].rearrange("p n t -> p (n t)").bitcast(I32) for g in range(PASSES)]
 
-        nc.sync.dma_start(slope_sb[0][:], slope_rows[:, 0, :])
-        nc.sync.dma_start(task_sb[:], task)
-        nc.sync.dma_start(slope_sb[1][:], slope_rows[:, 1, :])
+        xs_all = sbuf([P, T], U8, "xs_all")
+        xs_spread = sbuf([P, S], U8, "xs_spread")
+        xs_picked = sbuf([P, PASSES * S], U8, "xs_picked")
+        nc.vector.memset(xs_all[QUAD : 2 * QUAD, :].bitcast(I32), 0)
+        nc.vector.memset(xs_all[2 * QUAD :, :].bitcast(I32), 0)
+        nc.vector.memset(xs_picked[:].bitcast(I32), 0)
+
+        slope_sb = [sbuf([P, U], F32, "slope%d" % t) for t in range(PACK - 1)]
+        w1_raw = [sbuf([P, PACK, H], F32, "w1raw%d" % g) for g in range(PASSES)]
+
         nc.sync.dma_start(offs_sb[:], offs)
         nc.sync.dma_start(
-            xs_all[0:P:SPREAD, :, :].bitcast(I32), x_scales.rearrange("g b n -> b g n").bitcast(I32)
+            xs_all[:QUAD, :].bitcast(I32), x_scales.rearrange("g b n -> b g n").bitcast(I32)
         )
+        nc.sync.dma_start(slope_sb[0][:], slope_rows[:, 0, :])
+        nc.sync.dma_start(task_sb[:], task)
         nc.sync.dma_start(w1_raw[0][:], w1_rows[0])
-        for r in range(ROWS):
-            nc.sync.dma_start(
-                w2s_raw[r:P:QUAD, :].bitcast(I32), w2_scales[0].rearrange("(q r) n -> r q n", r=ROWS)[r].bitcast(I32)
-            )
+        nc.sync.dma_start(slope_sb[1][:], slope_rows[:, 1, :])
         nc.sync.dma_start(slope_sb[2][:], slope_rows[:, 2, :])
         nc.sync.dma_start(w1_raw[1][:], w1_rows[1])
-        nc.sync.dma_start(slope_sb[3][:], slope_rows[:, 3, :])
-        x_rows = [x_words[g].rearrange("p n t -> p (n t)").bitcast(I32) for g in range(PASSES)]
-        x_first = keep.tile([P, T], U32, name="x_first", tag="x_first", align_bytes=64)
-        nc.sync.dma_start(x_first[:].bitcast(I32), x_rows[0])
 
         def half_list(list_sb, h):
             return list_sb[:, HALF // GROUP * h : HALF // GROUP * (h + 1)]
 
-        picked_slope = keep.tile([P, PACK, S], F32, name="picked_slope", align_bytes=64)
+        picked_slope = sbuf([P, PACK, S], F32, "picked_slope")
 
         def pick_slopes(t):
             for h in range(S // HALF):
@@ -86,63 +82,68 @@ def tile_picked_prelu8_none_po_kernel(
                     picked_slope[:, t, HALF * h : HALF * (h + 1)], slope_sb[t][:].indirect(half_list(task_sb, h))
                 )
 
+        nc.vector.tensor_copy(xs_spread[:], xs_all[:].indirect(offs_sb[:]))
+        for q in range(QUADS):
+            nc.sync.dma_start(
+                xs_picked[QUAD * q + PLANE : QUAD * q + PLANE + ROWS, :].bitcast(I32).rearrange("p (g n) -> p g n", g=PASSES),
+                xs_spread[PASSES * ROWS * q : PASSES * ROWS * (q + 1), :].bitcast(I32),
+            )
+        slope_sb.append(sbuf([P, U], F32, "slope3", "xs_all"))
+        nc.sync.dma_start(slope_sb[3][:], slope_rows[:, 3, :])
         pick_slopes(0)
-        for g in range(PASSES):
-            nc.vector.tensor_copy(xs_spread[:, S * g : S * (g + 1)], xs_all[:, g, :].indirect(offs_sb[:]))
+        x_all = [sbuf([P, T], U32, "x_all0", "slope0")]
+        nc.sync.dma_start(x_all[0][:].bitcast(I32), x_rows[0])
+        pick_slopes(1)
+        w2s_raw = sbuf([P, N], U8, "w2s_raw", "slope1")
+        nc.vector.memset(w2s_raw[:].bitcast(I32), 0)
         for r in range(ROWS):
             nc.sync.dma_start(
-                xs_picked[PLANE + r : P : QUAD, :].bitcast(I32), xs_spread[SPREAD * r : P : QUAD, :].bitcast(I32)
+                w2s_raw[r:P:QUAD, :].bitcast(I32), w2_scales[0].rearrange("(q r) n -> r q n", r=ROWS)[r].bitcast(I32)
             )
-        x_last = keep.tile([P, T], U32, name="x_last", tag="xs_all", align_bytes=64)
-        nc.sync.dma_start(x_last[:].bitcast(I32), x_rows[1])
-        x_all = [x_first, x_last]
-        for t in range(1, PACK):
-            pick_slopes(t)
-        w2_raw = keep.tile([P, N], I32, name="w2_raw", tag="slope%d" % (PACK - 1), align_bytes=64)
-        nc.sync.dma_start(w2_raw[:], w2_words[0].rearrange("p n t -> p (n t)").bitcast(I32))
+        pick_slopes(2)
+        x_all.append(sbuf([P, T], U32, "x_all1", "slope2"))
+        nc.sync.dma_start(x_all[1][:].bitcast(I32), x_rows[1])
+        pick_slopes(3)
 
-        w1_codes = [
-            keep.tile([P, H], U32, name="w1codes%d" % g, tag="w1codes%d" % g, align_bytes=64) for g in range(PASSES)
-        ]
-        w1_scale = [keep.tile([P, H], U8, name="w1scale%d" % g, align_bytes=64) for g in range(PASSES)]
+        w1_codes = [sbuf([P, H], U32, "w1codes0"), sbuf([P, H], U32, "w1codes1", "xs_all")]
+        w1_scale = [sbuf([P, H], U8, "w1scale%d" % g) for g in range(PASSES)]
         for g in range(PASSES):
-            w1_bf = keep.tile([P, H * PACK], BF16, name="w1bf%d" % g, align_bytes=64)
+            w1_bf = sbuf([P, H * PACK], BF16, "w1bf%d" % g)
             dealt = w1_bf[:].rearrange("p (t m j) -> p m t j", t=PACK, j=PACK)
             raw = w1_raw[g][:].rearrange("p j (m t) -> p m t j", t=PACK)
-            on_scalar = P if g == 0 else 3 * P // 4
-            nc.scalar.activation(dealt[:, :on_scalar], raw[:, :on_scalar], ACT.Copy)
-            if on_scalar < P:
-                nc.vector.tensor_copy(dealt[:, on_scalar:], raw[:, on_scalar:])
+            nc.scalar.activation(dealt, raw, ACT.Copy)
             nc.vector.quantize_mx(out=w1_codes[g][:].bitcast(FP8X4), scales=w1_scale[g][:], in_=w1_bf[:])
 
-        woven_slope = keep.tile([P, S, PACK], F32, name="woven_slope", tag="w1raw%d" % (PASSES - 1), align_bytes=64)
+        w2_raw = sbuf([P, N], I32, "w2_raw", "w1raw1")
+        nc.sync.dma_start(w2_raw[:], w2_words[0].rearrange("p n t -> p (n t)").bitcast(I32))
+        woven_slope = [sbuf([P, CH, PACK], F32, "woven%d" % c) for c in range(NCH)]
         for c in range(NCH):
             cols = slice(CH * c, CH * (c + 1))
             nc.scalar.copy(
-                woven_slope[:, cols, :].rearrange("p (r i) t -> p r t i", i=RUN),
+                woven_slope[c][:].rearrange("p (r i) t -> p r t i", i=RUN),
                 picked_slope[:, :, cols].rearrange("p t (r i) -> p r t i", i=RUN),
             )
 
-        x_picked = [keep.tile([P, S], U32, name="xpicked%d" % g, align_bytes=64) for g in range(PASSES)]
+        x_picked = [sbuf([P, S], U32, "xpicked%d" % g) for g in range(PASSES)]
+        w2_scale = sbuf([P, N], U8, "w2_scale", "slope0")
         for g in range(PASSES):
             for h in range(S // HALF):
                 nc.vector.tensor_copy(
                     x_picked[g][:, HALF * h : HALF * (h + 1)], x_all[g][:].indirect(half_list(offs_sb, h))
                 )
+            if g == 0:
+                nc.vector.tensor_copy(
+                    w2_scale[:].rearrange("p (t m) -> p t m", t=PACK), w2s_raw[:].rearrange("p (m t) -> p t m", t=PACK)
+                )
 
-        w2_scale = keep.tile([P, N], U8, name="w2_scale", tag="x_first", align_bytes=64)
-        nc.vector.tensor_copy(
-            w2_scale[:].rearrange("p (t m) -> p t m", t=PACK), w2s_raw[:].rearrange("p (m t) -> p t m", t=PACK)
-        )
-
-        out_codes = keep.tile([P, S], U32, name="out_codes", align_bytes=64)
-        out_scale = keep.tile([P, S], U8, name="out_scale", align_bytes=64)
+        out_codes = sbuf([P, S], U32, "out_codes")
+        out_scale = sbuf([P, S], U8, "out_scale")
         out_rows = out_0.rearrange("(p t) s -> p t s", t=PACK)
         words_out = out_1[0].rearrange("p n t -> p (n t)").bitcast(I32)
 
         y = [psum.tile([P, PACK, CH], F32, name="y%d" % c, tag="y%d" % c) for c in range(NCH)]
-        z_codes = [keep.tile([P, CH], U32, name="zcodes%d" % c, align_bytes=64) for c in range(NCH)]
-        z_scale = [keep.tile([P, CH], U8, name="zscale%d" % c, align_bytes=64) for c in range(NCH)]
+        z_codes = [sbuf([P, CH], U32, "zcodes%d" % c) for c in range(NCH)]
+        z_scale = [sbuf([P, CH], U8, "zscale%d" % c) for c in range(NCH)]
 
         def first_product(c, t, g):
             cols = slice(CH * c, CH * (c + 1))
@@ -157,33 +158,41 @@ def tile_picked_prelu8_none_po_kernel(
                 stop=(g == PASSES - 1 and t == PACK - 1),
             )
 
-        above = [keep.tile([P, CH, PACK], BF16, name="above%d" % c, tag="above%d" % c, align_bytes=64) for c in range(NCH)]
-        below = [keep.tile([P, CH, PACK], BF16, name="below%d" % c, tag="below%d" % c, align_bytes=64) for c in range(NCH)]
-        z = [keep.tile([P, CH * PACK], BF16, name="z%d" % c, tag="z%d" % c, align_bytes=64) for c in range(NCH)]
-        res = [keep.tile([P, PACK, CH], F32, name="res%d" % c, align_bytes=64) for c in range(NCH)]
-        w2_codes = keep.tile([P, N], I32, name="w2_codes", align_bytes=64)
+        above = [sbuf([P, CH, PACK], BF16, "above%d" % c) for c in range(NCH)]
+        below = [sbuf([P, CH, PACK], BF16, "below%d" % c) for c in range(NCH)]
+        z = [sbuf([P, CH * PACK], BF16, "z%d" % c) for c in range(NCH)]
+        res = [sbuf([P, PACK, CH], F32, "res%d" % c) for c in range(NCH)]
         LAST = NCH - 1
-        res_tags = ["resbf0", "z%d" % LAST, "z%d" % (LAST - 1), "z%d" % (LAST - 2)]
-        res_bf = [
-            keep.tile([P, CH, PACK], BF16, name="resbf%d" % c, tag=res_tags[c], align_bytes=64) for c in range(NCH)
-        ]
+        res_tags = RES_TAGS
+        res_bf = [sbuf([P, CH, PACK], BF16, "resbf%d" % c, res_tags[c]) for c in range(NCH)]
 
         def keep_above(c):
             nc.scalar.activation(above[c][:], y[c][:].rearrange("p t n -> p n t"), ACT.Relu)
 
         def scale_below(c):
-            cols = slice(CH * c, CH * (c + 1))
             y_woven = y[c][:].rearrange("p t n -> p n t")
-            nc.vector.scalar_tensor_tensor(below[c][:], y_woven, 0.0, woven_slope[:, cols, :], ALU.min, ALU.mult)
+            nc.vector.scalar_tensor_tensor(below[c][:], y_woven, 0.0, woven_slope[c][:], ALU.min, ALU.mult)
 
         def join_signs(c):
             nc.vector.tensor_tensor(
                 z[c][:], above[c][:].rearrange("p n t -> p (n t)"), below[c][:].rearrange("p n t -> p (n t)"), ALU.add
             )
 
+        def add_above(c):
+            nc.vector.scalar_tensor_tensor(
+                z[c][:].rearrange("p (n t) -> p n t", t=PACK),
+                y[c][:].rearrange("p t n -> p n t"),
+                0.0,
+                below[c][:],
+                ALU.max,
+                ALU.add,
+            )
+
+        def quantize_z(c):
+            nc.vector.quantize_mx(out=z_codes[c][:].bitcast(FP8X4), scales=z_scale[c][:], in_=z[c][:])
+
         def second_product(c):
             cols = slice(CH * c, CH * (c + 1))
-            nc.vector.quantize_mx(out=z_codes[c][:].bitcast(FP8X4), scales=z_scale[c][:], in_=z[c][:])
             parts = 2 if c == LAST else 1
             width = PACK // parts
             for part in range(parts):
@@ -207,7 +216,7 @@ def tile_picked_prelu8_none_po_kernel(
             nc.sync.dma_start(out_rows[:, :, cols], res[c][:])
 
         def round_out(c):
-            weave = nc.scalar.copy if c == 0 else nc.vector.tensor_copy
+            weave = nc.scalar.copy if c in ROUND_ON_SCALAR else nc.vector.tensor_copy
             weave(
                 res_bf[c][:].rearrange("p (r i) t -> p r t i", i=RUN),
                 res[c][:].rearrange("p t (r i) -> p r t i", i=RUN),
@@ -220,37 +229,47 @@ def tile_picked_prelu8_none_po_kernel(
                 scales=out_scale[:, cols],
                 in_=res_bf[c][:].rearrange("p n t -> p (n t)"),
             )
-            if c % 2 == 1:
-                pair = slice(CH * (c - 1), CH * (c + 1))
+            if c in (1, 2):
+                pair = slice(2 * CH * (c - 1), 2 * CH * c)
                 nc.sync.dma_start(words_out[:, pair], out_codes[:, pair].bitcast(I32))
 
         for g in range(PASSES):
             for c in range(NCH):
                 for t in range(PACK):
                     first_product(c, t, g)
+        w2_codes = sbuf([P, N], I32, "w2_codes")
         nc.vector.tensor_copy(
             w2_codes[:].rearrange("p (t r i) -> p r t i", t=PACK, i=RUN),
             w2_raw[:].rearrange("p (r i t) -> p r t i", t=PACK, i=RUN),
         )
-        for c in range(NCH):
-            if c == 0:
-                scale_below(c)
-                nc.vector.scalar_tensor_tensor(
-                    z[c][:].rearrange("p (n t) -> p n t", t=PACK),
-                    y[c][:].rearrange("p t n -> p n t"),
-                    0.0,
-                    below[c][:],
-                    ALU.max,
-                    ALU.add,
-                )
-            else:
-                keep_above(c)
-                scale_below(c)
-                join_signs(c)
-            second_product(c)
-        for c in range(NCH):
-            round_out(c)
-            quantize_out(c)
+        scale_below(0)
+        keep_above(1)
+        scale_below(2)
+        keep_above(0)
+        scale_below(1)
+        keep_above(3)
+        join_signs(0)
+        keep_above(2)
+        join_signs(1)
+        quantize_z(0)
+        second_product(0)
+        scale_below(3)
+        quantize_z(1)
+        second_product(1)
+        join_signs(2)
+        join_signs(3)
+        quantize_z(2)
+        quantize_z(3)
+        second_product(2)
+        second_product(3)
+        round_out(0)
+        round_out(1)
+        quantize_out(0)
+        quantize_out(1)
+        round_out(3)
+        round_out(2)
+        quantize_out(3)
+        quantize_out(2)
         for r in range(ROWS):
             queue = nc.sync if r % 2 == 0 else nc.scalar
             queue.dma_start(

@@ -31,6 +31,7 @@ RUN = 4
 XSTEP = 4
 RES_TAGS = ["z2", "z3", "resbf2", "resbf3"]
 ROUND_ON_SCALAR = (2,)
+ON_SCALAR = 128
 
 
 def tile_picked_prelu8_none_po_kernel(
@@ -60,12 +61,12 @@ def tile_picked_prelu8_none_po_kernel(
         slope_sb = [sbuf([P, U], F32, "slope%d" % t) for t in range(PACK - 1)]
         w1_raw = [sbuf([P, PACK, H], F32, "w1raw%d" % g) for g in range(PASSES)]
 
-        nc.sync.dma_start(offs_sb[:], offs)
+        nc.sync.dma_start(slope_sb[0][:], slope_rows[:, 0, :])
+        nc.sync.dma_start(task_sb[:], task)
         nc.sync.dma_start(
             xs_all[:QUAD, :].bitcast(I32), x_scales.rearrange("g b n -> b g n").bitcast(I32)
         )
-        nc.sync.dma_start(slope_sb[0][:], slope_rows[:, 0, :])
-        nc.sync.dma_start(task_sb[:], task)
+        nc.sync.dma_start(offs_sb[:], offs)
         nc.sync.dma_start(w1_raw[0][:], w1_rows[0])
         nc.sync.dma_start(slope_sb[1][:], slope_rows[:, 1, :])
         nc.sync.dma_start(slope_sb[2][:], slope_rows[:, 2, :])
@@ -107,14 +108,22 @@ def tile_picked_prelu8_none_po_kernel(
 
         w1_codes = [sbuf([P, H], U32, "w1codes0"), sbuf([P, H], U32, "w1codes1", "xs_all")]
         w1_scale = [sbuf([P, H], U8, "w1scale%d" % g) for g in range(PASSES)]
+        w1_bf = [sbuf([P, H * PACK], BF16, "w1bf%d" % g) for g in range(PASSES)]
         for g in range(PASSES):
-            w1_bf = sbuf([P, H * PACK], BF16, "w1bf%d" % g)
-            dealt = w1_bf[:].rearrange("p (t m j) -> p m t j", t=PACK, j=PACK)
-            raw = w1_raw[g][:].rearrange("p j (m t) -> p m t j", t=PACK)
-            nc.scalar.activation(dealt, raw, ACT.Copy)
-            nc.vector.quantize_mx(out=w1_codes[g][:].bitcast(FP8X4), scales=w1_scale[g][:], in_=w1_bf[:])
+            dealt = w1_bf[g][:].rearrange("p (t m j) -> p m j t", t=PACK, j=PACK)
+            raw = w1_raw[g][:].rearrange("p j (m t) -> p m j t", t=PACK)
+            on_scalar = P if g == 0 else ON_SCALAR
+            nc.scalar.activation(dealt[:, :on_scalar], raw[:, :on_scalar], ACT.Copy)
+            if on_scalar < P:
+                nc.vector.tensor_copy(dealt[:, on_scalar:], raw[:, on_scalar:])
 
-        w2_raw = sbuf([P, N], I32, "w2_raw", "w1raw1")
+        def quantize_w1(g):
+            nc.vector.quantize_mx(out=w1_codes[g][:].bitcast(FP8X4), scales=w1_scale[g][:], in_=w1_bf[g][:])
+
+        quantize_w1(0)
+        quantize_w1(1)
+
+        w2_raw = sbuf([P, N], I32, "w2_raw", "w1raw0")
         nc.sync.dma_start(w2_raw[:], w2_words[0].rearrange("p n t -> p (n t)").bitcast(I32))
         woven_slope = [sbuf([P, CH, PACK], F32, "woven%d" % c) for c in range(NCH)]
         for c in range(NCH):
@@ -125,13 +134,13 @@ def tile_picked_prelu8_none_po_kernel(
             )
 
         x_picked = [sbuf([P, S], U32, "xpicked%d" % g) for g in range(PASSES)]
-        w2_scale = sbuf([P, N], U8, "w2_scale", "slope0")
         for g in range(PASSES):
             for h in range(S // HALF):
                 nc.vector.tensor_copy(
                     x_picked[g][:, HALF * h : HALF * (h + 1)], x_all[g][:].indirect(half_list(offs_sb, h))
                 )
             if g == 0:
+                w2_scale = sbuf([P, N], U8, "w2_scale", "slope0")
                 nc.vector.tensor_copy(
                     w2_scale[:].rearrange("p (t m) -> p t m", t=PACK), w2s_raw[:].rearrange("p (m t) -> p t m", t=PACK)
                 )

@@ -95,18 +95,12 @@ def tile_picked_prelu8_none_po_kernel(
         x_all = [sbuf([P, T], U32, "x_all0", "slope0")]
         nc.sync.dma_start(x_all[0][:].bitcast(I32), x_rows[0])
         pick_slopes(1)
-        w2s_raw = sbuf([P, N], U8, "w2s_raw", "slope1")
-        nc.vector.memset(w2s_raw[:].bitcast(I32), 0)
-        for r in range(ROWS):
-            nc.sync.dma_start(
-                w2s_raw[r:P:QUAD, :].bitcast(I32), w2_scales[0].rearrange("(q r) n -> r q n", r=ROWS)[r].bitcast(I32)
-            )
-        pick_slopes(2)
-        x_all.append(sbuf([P, T], U32, "x_all1", "slope2"))
+        x_all.append(sbuf([P, T], U32, "x_all1", "slope1"))
         nc.sync.dma_start(x_all[1][:].bitcast(I32), x_rows[1])
+        pick_slopes(2)
         pick_slopes(3)
 
-        w1_codes = [sbuf([P, H], U32, "w1codes0"), sbuf([P, H], U32, "w1codes1", "xs_all")]
+        w1_codes = [sbuf([P, H], U32, "w1codes0")]
         w1_scale = [sbuf([P, H], U8, "w1scale%d" % g) for g in range(PASSES)]
         w1_bf = [sbuf([P, H * PACK], BF16, "w1bf%d" % g) for g in range(PASSES)]
         for g in range(PASSES):
@@ -121,10 +115,15 @@ def tile_picked_prelu8_none_po_kernel(
             nc.vector.quantize_mx(out=w1_codes[g][:].bitcast(FP8X4), scales=w1_scale[g][:], in_=w1_bf[g][:])
 
         quantize_w1(0)
-        quantize_w1(1)
 
         w2_raw = sbuf([P, N], I32, "w2_raw", "w1raw0")
         nc.sync.dma_start(w2_raw[:], w2_words[0].rearrange("p n t -> p (n t)").bitcast(I32))
+        w2s_raw = sbuf([P, N], U8, "w2s_raw", "slope2")
+        nc.vector.memset(w2s_raw[:].bitcast(I32), 0)
+        for r in range(ROWS):
+            nc.sync.dma_start(
+                w2s_raw[r:P:QUAD, :].bitcast(I32), w2_scales[0].rearrange("(q r) n -> r q n", r=ROWS)[r].bitcast(I32)
+            )
         woven_slope = [sbuf([P, CH, PACK], F32, "woven%d" % c) for c in range(NCH)]
         for c in range(NCH):
             cols = slice(CH * c, CH * (c + 1))
@@ -140,10 +139,8 @@ def tile_picked_prelu8_none_po_kernel(
                     x_picked[g][:, HALF * h : HALF * (h + 1)], x_all[g][:].indirect(half_list(offs_sb, h))
                 )
             if g == 0:
-                w2_scale = sbuf([P, N], U8, "w2_scale", "slope0")
-                nc.vector.tensor_copy(
-                    w2_scale[:].rearrange("p (t m) -> p t m", t=PACK), w2s_raw[:].rearrange("p (m t) -> p t m", t=PACK)
-                )
+                w1_codes.append(sbuf([P, H], U32, "w1codes1", "slope0"))
+                quantize_w1(1)
 
         out_codes = sbuf([P, S], U32, "out_codes")
         out_scale = sbuf([P, S], U8, "out_scale")
@@ -246,10 +243,13 @@ def tile_picked_prelu8_none_po_kernel(
             for c in range(NCH):
                 for t in range(PACK):
                     first_product(c, t, g)
-        w2_codes = sbuf([P, N], I32, "w2_codes")
-        nc.vector.tensor_copy(
-            w2_codes[:].rearrange("p (t r i) -> p r t i", t=PACK, i=RUN),
-            w2_raw[:].rearrange("p (r i t) -> p r t i", t=PACK, i=RUN),
+        w2_codes = sbuf([P, N], I32, "w2_codes", "slope1")
+        nc.gpsimd.tensor_copy(
+            w2_codes[:].rearrange("p (t m) -> p t m", t=PACK), w2_raw[:].rearrange("p (m t) -> p t m", t=PACK)
+        )
+        w2_scale = sbuf([P, N], U8, "w2_scale", "w1raw0")
+        nc.gpsimd.tensor_copy(
+            w2_scale[:].rearrange("p (t m) -> p t m", t=PACK), w2s_raw[:].rearrange("p (m t) -> p t m", t=PACK)
         )
         scale_below(0)
         keep_above(1)

@@ -255,6 +255,17 @@ def tile_picked_prelu8_none_po_kernel(
         keep_above(1)
         scale_below(2)
         keep_above(0)
+        warm = psum.tile([P, H], F32, name="warm", tag="y0")
+        for i in range(2):
+            nc.tensor.matmul_mx(
+                out=warm[:],
+                lhsT=w1_codes[0][:, :P].bitcast(FP8X4),
+                lhsT_scale=w1_scale[0][:, :P],
+                rhs=w1_codes[0][:].bitcast(FP8X4),
+                rhs_scale=w1_scale[0][:],
+                start=True,
+                stop=True,
+            )
         scale_below(1)
         keep_above(3)
         join_signs(0)
@@ -262,6 +273,17 @@ def tile_picked_prelu8_none_po_kernel(
         join_signs(1)
         quantize_z(0)
         second_product(0)
+        warm_late = psum.tile([P, H], F32, name="warm_late", tag="y1")
+        for i in range(1):
+            nc.tensor.matmul_mx(
+                out=warm_late[:],
+                lhsT=w1_codes[0][:, :P].bitcast(FP8X4),
+                lhsT_scale=w1_scale[0][:, :P],
+                rhs=w1_codes[0][:].bitcast(FP8X4),
+                rhs_scale=w1_scale[0][:],
+                start=True,
+                stop=True,
+            )
         scale_below(3)
         quantize_z(1)
         second_product(1)

@@ -30,8 +30,8 @@ HALF = S // 2
 RUN = 4
 XSTEP = 4
 RES_TAGS = ["z2", "z3", "resbf2", "resbf3"]
-ROUND_ON_SCALAR = (2,)
-ON_SCALAR = 128
+ROUND_SHARED = (0, 3)
+SHARED_RUNS = 16
 
 
 def tile_picked_prelu8_none_po_kernel(
@@ -75,13 +75,22 @@ def tile_picked_prelu8_none_po_kernel(
         def half_list(list_sb, h):
             return list_sb[:, HALF // GROUP * h : HALF // GROUP * (h + 1)]
 
-        picked_slope = sbuf([P, PACK, S], F32, "picked_slope")
+        low_slope = sbuf([P, 2, S], F32, "low_slope")
+        high_slope = [sbuf([P, 2, CH], F32, "high_slope%d" % c) for c in range(NCH)]
 
         def pick_slopes(t):
-            for h in range(S // HALF):
-                nc.vector.tensor_copy(
-                    picked_slope[:, t, HALF * h : HALF * (h + 1)], slope_sb[t][:].indirect(half_list(task_sb, h))
-                )
+            if t < 2:
+                for h in range(S // HALF):
+                    nc.vector.tensor_copy(
+                        low_slope[:, t, HALF * h : HALF * (h + 1)], slope_sb[t][:].indirect(half_list(task_sb, h))
+                    )
+            else:
+                for c in range(NCH):
+                    window = slope_sb[t][:].indirect(task_sb[:, CH // GROUP * c : CH // GROUP * (c + 1)])
+                    if t == PACK - 1:
+                        nc.scalar.activation(high_slope[c][:, 1, :], window, ACT.Copy)
+                    else:
+                        nc.vector.tensor_copy(high_slope[c][:, 0, :], window)
 
         nc.vector.tensor_copy(xs_spread[:], xs_all[:].indirect(offs_sb[:]))
         for q in range(QUADS):
@@ -89,8 +98,6 @@ def tile_picked_prelu8_none_po_kernel(
                 xs_picked[QUAD * q + PLANE : QUAD * q + PLANE + ROWS, :].bitcast(I32).rearrange("p (g n) -> p g n", g=PASSES),
                 xs_spread[PASSES * ROWS * q : PASSES * ROWS * (q + 1), :].bitcast(I32),
             )
-        slope_sb.append(sbuf([P, U], F32, "slope3", "xs_all"))
-        nc.sync.dma_start(slope_sb[3][:], slope_rows[:, 3, :])
         pick_slopes(0)
         x_all = [sbuf([P, T], U32, "x_all0", "slope0")]
         nc.sync.dma_start(x_all[0][:].bitcast(I32), x_rows[0])
@@ -98,7 +105,8 @@ def tile_picked_prelu8_none_po_kernel(
         x_all.append(sbuf([P, T], U32, "x_all1", "slope1"))
         nc.sync.dma_start(x_all[1][:].bitcast(I32), x_rows[1])
         pick_slopes(2)
-        pick_slopes(3)
+        slope_sb.append(sbuf([P, U], F32, "slope3", "slope2"))
+        nc.sync.dma_start(slope_sb[3][:], slope_rows[:, 3, :])
 
         w1_codes = [sbuf([P, H], U32, "w1codes0")]
         w1_scale = [sbuf([P, H], U8, "w1scale%d" % g) for g in range(PASSES)]
@@ -106,10 +114,7 @@ def tile_picked_prelu8_none_po_kernel(
         for g in range(PASSES):
             dealt = w1_bf[g][:].rearrange("p (t m j) -> p m j t", t=PACK, j=PACK)
             raw = w1_raw[g][:].rearrange("p j (m t) -> p m j t", t=PACK)
-            on_scalar = P if g == 0 else ON_SCALAR
-            nc.scalar.activation(dealt[:, :on_scalar], raw[:, :on_scalar], ACT.Copy)
-            if on_scalar < P:
-                nc.vector.tensor_copy(dealt[:, on_scalar:], raw[:, on_scalar:])
+            nc.scalar.activation(dealt, raw, ACT.Copy)
 
         def quantize_w1(g):
             nc.vector.quantize_mx(out=w1_codes[g][:].bitcast(FP8X4), scales=w1_scale[g][:], in_=w1_bf[g][:])
@@ -118,29 +123,21 @@ def tile_picked_prelu8_none_po_kernel(
 
         w2_raw = sbuf([P, N], I32, "w2_raw", "w1raw0")
         nc.sync.dma_start(w2_raw[:], w2_words[0].rearrange("p n t -> p (n t)").bitcast(I32))
-        w2s_raw = sbuf([P, N], U8, "w2s_raw", "slope2")
+        w2s_raw = sbuf([P, N], U8, "w2s_raw", "w1bf0")
         nc.vector.memset(w2s_raw[:].bitcast(I32), 0)
         for r in range(ROWS):
             nc.sync.dma_start(
                 w2s_raw[r:P:QUAD, :].bitcast(I32), w2_scales[0].rearrange("(q r) n -> r q n", r=ROWS)[r].bitcast(I32)
             )
-        woven_slope = [sbuf([P, CH, PACK], F32, "woven%d" % c) for c in range(NCH)]
-        for c in range(NCH):
-            cols = slice(CH * c, CH * (c + 1))
-            nc.scalar.copy(
-                woven_slope[c][:].rearrange("p (r i) t -> p r t i", i=RUN),
-                picked_slope[:, :, cols].rearrange("p t (r i) -> p r t i", i=RUN),
-            )
-
         x_picked = [sbuf([P, S], U32, "xpicked%d" % g) for g in range(PASSES)]
+        cuts = [[0, HALF, S], [0, CH, HALF, S]]
         for g in range(PASSES):
-            for h in range(S // HALF):
-                nc.vector.tensor_copy(
-                    x_picked[g][:, HALF * h : HALF * (h + 1)], x_all[g][:].indirect(half_list(offs_sb, h))
-                )
+            for a, b in zip(cuts[g], cuts[g][1:]):
+                nc.vector.tensor_copy(x_picked[g][:, a:b], x_all[g][:].indirect(offs_sb[:, a // GROUP : b // GROUP]))
             if g == 0:
                 w1_codes.append(sbuf([P, H], U32, "w1codes1", "slope0"))
                 quantize_w1(1)
+        pick_slopes(3)
 
         out_codes = sbuf([P, S], U32, "out_codes")
         out_scale = sbuf([P, S], U8, "out_scale")
@@ -151,7 +148,7 @@ def tile_picked_prelu8_none_po_kernel(
         z_codes = [sbuf([P, CH], U32, "zcodes%d" % c) for c in range(NCH)]
         z_scale = [sbuf([P, CH], U8, "zscale%d" % c) for c in range(NCH)]
 
-        def first_product(c, t, g):
+        def first_product(c, t, g, first, last):
             cols = slice(CH * c, CH * (c + 1))
             feats = slice(P * t, P * (t + 1))
             nc.tensor.matmul_mx(
@@ -160,37 +157,40 @@ def tile_picked_prelu8_none_po_kernel(
                 lhsT_scale=w1_scale[g][:, feats],
                 rhs=x_picked[g][:, cols].bitcast(FP8X4),
                 rhs_scale=xs_picked[PLANE:P, S * g + CH * c : S * g + CH * (c + 1)],
-                start=(g == 0 and t == 0),
-                stop=(g == PASSES - 1 and t == PACK - 1),
+                start=(g == first and t == 0),
+                stop=(g == last and t == PACK - 1),
             )
 
-        above = [sbuf([P, CH, PACK], BF16, "above%d" % c) for c in range(NCH)]
-        below = [sbuf([P, CH, PACK], BF16, "below%d" % c) for c in range(NCH)]
+        above = {}
+        below = {}
         z = [sbuf([P, CH * PACK], BF16, "z%d" % c) for c in range(NCH)]
         res = [sbuf([P, PACK, CH], F32, "res%d" % c) for c in range(NCH)]
         LAST = NCH - 1
         res_tags = RES_TAGS
         res_bf = [sbuf([P, CH, PACK], BF16, "resbf%d" % c, res_tags[c]) for c in range(NCH)]
 
-        def keep_above(c):
+        def keep_above(c, takes_over=None):
+            above[c] = sbuf([P, CH, PACK], BF16, "above%d" % c, takes_over)
             nc.scalar.activation(above[c][:], y[c][:].rearrange("p t n -> p n t"), ACT.Relu)
 
-        def scale_below(c):
-            y_woven = y[c][:].rearrange("p t n -> p n t")
-            nc.vector.scalar_tensor_tensor(below[c][:], y_woven, 0.0, woven_slope[c][:], ALU.min, ALU.mult)
+        def scale_below(c, takes_over=None):
+            below[c] = sbuf([P, 2, CH, 2], BF16, "below%d" % c, takes_over)
+            pairs = [low_slope[:, :, CH * c : CH * (c + 1)], high_slope[c][:]]
+            for u in range(2):
+                nc.vector.scalar_tensor_tensor(
+                    below[c][:, u],
+                    y[c][:, 2 * u : 2 * u + 2, :].rearrange("p e n -> p n e"),
+                    0.0,
+                    pairs[u].rearrange("p e n -> p n e"),
+                    ALU.min,
+                    ALU.mult,
+                )
 
         def join_signs(c):
             nc.vector.tensor_tensor(
-                z[c][:], above[c][:].rearrange("p n t -> p (n t)"), below[c][:].rearrange("p n t -> p (n t)"), ALU.add
-            )
-
-        def add_above(c):
-            nc.vector.scalar_tensor_tensor(
-                z[c][:].rearrange("p (n t) -> p n t", t=PACK),
-                y[c][:].rearrange("p t n -> p n t"),
-                0.0,
-                below[c][:],
-                ALU.max,
+                z[c][:].rearrange("p (n u e) -> p n u e", u=2, e=2),
+                above[c][:].rearrange("p n (u e) -> p n u e", u=2),
+                below[c][:].rearrange("p u n e -> p n u e"),
                 ALU.add,
             )
 
@@ -199,34 +199,28 @@ def tile_picked_prelu8_none_po_kernel(
 
         def second_product(c):
             cols = slice(CH * c, CH * (c + 1))
-            parts = 2 if c == LAST else 1
-            width = PACK // parts
-            for part in range(parts):
-                tag = "acc%d" % c if part == 0 else "y0"
-                acc = psum.tile([P, width, CH], F32, name="acc%d_%d" % (c, part), tag=tag)
-                for i in range(width):
-                    dealt_cols = slice(P * (width * part + i), P * (width * part + i + 1))
-                    nc.tensor.matmul_mx(
-                        out=acc[:, i, :],
-                        lhsT=w2_codes[:, dealt_cols].bitcast(FP8X4),
-                        lhsT_scale=w2_scale[:, dealt_cols],
-                        rhs=z_codes[c][:].bitcast(FP8X4),
-                        rhs_scale=z_scale[c][:],
-                        start=True,
-                        stop=True,
-                    )
-                if part == 0:
-                    nc.scalar.copy(res[c][:, :width, :], acc[:])
-                else:
-                    nc.vector.tensor_copy(res[c][:, width:, :], acc[:])
+            acc = psum.tile([P, PACK, CH], F32, name="acc%d" % c, tag="acc%d" % c)
+            for t in range(PACK):
+                dealt_cols = slice(P * t, P * (t + 1))
+                nc.tensor.matmul_mx(
+                    out=acc[:, t, :],
+                    lhsT=w2_codes[:, dealt_cols].bitcast(FP8X4),
+                    lhsT_scale=w2_scale[:, dealt_cols],
+                    rhs=z_codes[c][:].bitcast(FP8X4),
+                    rhs_scale=z_scale[c][:],
+                    start=True,
+                    stop=True,
+                )
+            nc.scalar.copy(res[c][:], acc[:])
             nc.sync.dma_start(out_rows[:, :, cols], res[c][:])
 
         def round_out(c):
-            weave = nc.scalar.copy if c in ROUND_ON_SCALAR else nc.vector.tensor_copy
-            weave(
-                res_bf[c][:].rearrange("p (r i) t -> p r t i", i=RUN),
-                res[c][:].rearrange("p t (r i) -> p r t i", i=RUN),
-            )
+            woven = res_bf[c][:].rearrange("p (r i) t -> p r t i", i=RUN)
+            plain = res[c][:].rearrange("p t (r i) -> p r t i", i=RUN)
+            shared = SHARED_RUNS if c in ROUND_SHARED else 0
+            if shared:
+                nc.scalar.copy(woven[:, :shared], plain[:, :shared])
+            nc.vector.tensor_copy(woven[:, shared:], plain[:, shared:])
 
         def quantize_out(c):
             cols = slice(CH * c, CH * (c + 1))
@@ -235,14 +229,17 @@ def tile_picked_prelu8_none_po_kernel(
                 scales=out_scale[:, cols],
                 in_=res_bf[c][:].rearrange("p n t -> p (n t)"),
             )
-            if c in (1, 2):
-                pair = slice(2 * CH * (c - 1), 2 * CH * c)
+            if c in (1, 3):
+                pair = slice(CH * (c - 1), CH * (c + 1))
                 nc.sync.dma_start(words_out[:, pair], out_codes[:, pair].bitcast(I32))
 
         for g in range(PASSES):
-            for c in range(NCH):
+            for c in range(LAST):
                 for t in range(PACK):
-                    first_product(c, t, g)
+                    first_product(c, t, g, 0, 1)
+        for g in (1, 0):
+            for t in range(PACK):
+                first_product(LAST, t, g, 1, 0)
         w2_codes = sbuf([P, N], I32, "w2_codes", "slope1")
         nc.gpsimd.tensor_copy(
             w2_codes[:].rearrange("p (t m) -> p t m", t=PACK), w2_raw[:].rearrange("p (m t) -> p t m", t=PACK)
@@ -252,41 +249,19 @@ def tile_picked_prelu8_none_po_kernel(
             w2_scale[:].rearrange("p (t m) -> p t m", t=PACK), w2s_raw[:].rearrange("p (m t) -> p t m", t=PACK)
         )
         scale_below(0)
-        keep_above(1)
-        scale_below(2)
         keep_above(0)
-        warm = psum.tile([P, H], F32, name="warm", tag="y0")
-        for i in range(2):
-            nc.tensor.matmul_mx(
-                out=warm[:],
-                lhsT=w1_codes[0][:, :P].bitcast(FP8X4),
-                lhsT_scale=w1_scale[0][:, :P],
-                rhs=w1_codes[0][:].bitcast(FP8X4),
-                rhs_scale=w1_scale[0][:],
-                start=True,
-                stop=True,
-            )
         scale_below(1)
-        keep_above(3)
+        keep_above(1)
+        scale_below(2, "high_slope0")
+        keep_above(3, "high_slope1")
         join_signs(0)
-        keep_above(2)
         join_signs(1)
+        keep_above(2, "above1")
         quantize_z(0)
-        second_product(0)
-        warm_late = psum.tile([P, H], F32, name="warm_late", tag="y1")
-        for i in range(1):
-            nc.tensor.matmul_mx(
-                out=warm_late[:],
-                lhsT=w1_codes[0][:, :P].bitcast(FP8X4),
-                lhsT_scale=w1_scale[0][:, :P],
-                rhs=w1_codes[0][:].bitcast(FP8X4),
-                rhs_scale=w1_scale[0][:],
-                start=True,
-                stop=True,
-            )
-        scale_below(3)
         quantize_z(1)
+        second_product(0)
         second_product(1)
+        scale_below(3, "below1")
         join_signs(2)
         join_signs(3)
         quantize_z(2)
@@ -297,10 +272,10 @@ def tile_picked_prelu8_none_po_kernel(
         round_out(1)
         quantize_out(0)
         quantize_out(1)
-        round_out(3)
         round_out(2)
-        quantize_out(3)
+        round_out(3)
         quantize_out(2)
+        quantize_out(3)
         for r in range(ROWS):
             queue = nc.sync if r % 2 == 0 else nc.scalar
             queue.dma_start(

@@ -58,19 +58,23 @@ def tile_picked_prelu8_none_po_kernel(
         nc.vector.memset(xs_all[2 * QUAD :, :].bitcast(I32), 0)
         nc.vector.memset(xs_picked[:].bitcast(I32), 0)
 
-        slope_sb = [sbuf([P, U], F32, "slope%d" % t) for t in range(PACK - 1)]
+        early_slopes = sbuf([P, (PACK - 1) * U], F32, "early_slopes")
         w1_raw = [sbuf([P, PACK, H], F32, "w1raw%d" % g) for g in range(PASSES)]
 
-        nc.sync.dma_start(slope_sb[0][:], slope_rows[:, 0, :])
-        nc.sync.dma_start(task_sb[:], task)
+        x_all = [sbuf([P, T], U32, "x_all0")]
+        nc.sync.dma_start(early_slopes[:], slope.rearrange("(p t) u -> p (t u)", t=PACK)[:, : (PACK - 1) * U])
         nc.sync.dma_start(
             xs_all[:QUAD, :].bitcast(I32), x_scales.rearrange("g b n -> b g n").bitcast(I32)
         )
         nc.sync.dma_start(offs_sb[:], offs)
+        nc.sync.dma_start(task_sb[:], task)
         nc.sync.dma_start(w1_raw[0][:], w1_rows[0])
-        nc.sync.dma_start(slope_sb[1][:], slope_rows[:, 1, :])
-        nc.sync.dma_start(slope_sb[2][:], slope_rows[:, 2, :])
         nc.sync.dma_start(w1_raw[1][:], w1_rows[1])
+        nc.sync.dma_start(x_all[0][:].bitcast(I32), x_rows[0])
+        slope_sb = [early_slopes]
+        for t in range(1, PACK - 1):
+            slope_sb.append(sbuf([P, U], F32, "slope%d" % t))
+            nc.scalar.copy(slope_sb[t][:], early_slopes[:, U * t : U * (t + 1)])
 
         def half_list(list_sb, h):
             return list_sb[:, HALF // GROUP * h : HALF // GROUP * (h + 1)]
@@ -79,7 +83,9 @@ def tile_picked_prelu8_none_po_kernel(
         high_slope = [sbuf([P, 2, CH], F32, "high_slope%d" % c) for c in range(NCH)]
 
         def pick_slopes(t):
-            if t < 2:
+            if t == 0:
+                nc.vector.tensor_copy(low_slope[:, 0, :], early_slopes[:].indirect(task_sb[:]))
+            elif t == 1:
                 for h in range(S // HALF):
                     nc.vector.tensor_copy(
                         low_slope[:, t, HALF * h : HALF * (h + 1)], slope_sb[t][:].indirect(half_list(task_sb, h))
@@ -94,19 +100,17 @@ def tile_picked_prelu8_none_po_kernel(
 
         nc.vector.tensor_copy(xs_spread[:], xs_all[:].indirect(offs_sb[:]))
         for q in range(QUADS):
-            nc.sync.dma_start(
+            nc.scalar.dma_start(
                 xs_picked[QUAD * q + PLANE : QUAD * q + PLANE + ROWS, :].bitcast(I32).rearrange("p (g n) -> p g n", g=PASSES),
                 xs_spread[PASSES * ROWS * q : PASSES * ROWS * (q + 1), :].bitcast(I32),
             )
         pick_slopes(0)
-        x_all = [sbuf([P, T], U32, "x_all0", "slope0")]
-        nc.sync.dma_start(x_all[0][:].bitcast(I32), x_rows[0])
-        pick_slopes(1)
-        x_all.append(sbuf([P, T], U32, "x_all1", "slope1"))
+        x_all.append(sbuf([P, T], U32, "x_all1", "early_slopes"))
         nc.sync.dma_start(x_all[1][:].bitcast(I32), x_rows[1])
-        pick_slopes(2)
-        slope_sb.append(sbuf([P, U], F32, "slope3", "slope2"))
+        pick_slopes(1)
+        slope_sb.append(sbuf([P, U], F32, "slope3", "slope1"))
         nc.sync.dma_start(slope_sb[3][:], slope_rows[:, 3, :])
+        pick_slopes(2)
 
         w1_codes = [sbuf([P, H], U32, "w1codes0")]
         w1_scale = [sbuf([P, H], U8, "w1scale%d" % g) for g in range(PASSES)]
@@ -135,7 +139,7 @@ def tile_picked_prelu8_none_po_kernel(
             for a, b in zip(cuts[g], cuts[g][1:]):
                 nc.vector.tensor_copy(x_picked[g][:, a:b], x_all[g][:].indirect(offs_sb[:, a // GROUP : b // GROUP]))
             if g == 0:
-                w1_codes.append(sbuf([P, H], U32, "w1codes1", "slope0"))
+                w1_codes.append(sbuf([P, H], U32, "w1codes1", "x_all0"))
                 quantize_w1(1)
         pick_slopes(3)
 
@@ -240,7 +244,7 @@ def tile_picked_prelu8_none_po_kernel(
         for g in (1, 0):
             for t in range(PACK):
                 first_product(LAST, t, g, 1, 0)
-        w2_codes = sbuf([P, N], I32, "w2_codes", "slope1")
+        w2_codes = sbuf([P, N], I32, "w2_codes", "early_slopes")
         nc.gpsimd.tensor_copy(
             w2_codes[:].rearrange("p (t m) -> p t m", t=PACK), w2_raw[:].rearrange("p (m t) -> p t m", t=PACK)
         )

@@ -233,9 +233,6 @@ def tile_picked_prelu8_none_po_kernel(
                 scales=out_scale[:, cols],
                 in_=res_bf[c][:].rearrange("p n t -> p (n t)"),
             )
-            if c in (1, 3):
-                pair = slice(CH * (c - 1), CH * (c + 1))
-                nc.sync.dma_start(words_out[:, pair], out_codes[:, pair].bitcast(I32))
 
         for g in range(PASSES):
             for c in range(LAST):
@@ -280,8 +277,9 @@ def tile_picked_prelu8_none_po_kernel(
         round_out(3)
         quantize_out(2)
         quantize_out(3)
+        nc.sync.dma_start(words_out, out_codes[:].bitcast(I32))
         for r in range(ROWS):
-            queue = nc.sync if r % 2 == 0 else nc.scalar
+            queue = nc.scalar if r % 2 == 0 else nc.sync
             queue.dma_start(
                 out_2[0].rearrange("(q r) n -> r q n", r=ROWS)[r].bitcast(I32),
                 out_scale[r:P:QUAD, :].bitcast(I32),

@@ -30,8 +30,8 @@ HALF = S // 2
 RUN = 4
 XSTEP = 4
 RES_TAGS = ["z2", "z3", "resbf2", "resbf3"]
-ROUND_SHARED = (0, 3)
-SHARED_RUNS = 16
+ON_SCALAR = (64, 0, 0, 80)
+CAST_ON_SCALAR = 96
 
 
 def tile_picked_prelu8_none_po_kernel(
@@ -118,7 +118,10 @@ def tile_picked_prelu8_none_po_kernel(
         for g in range(PASSES):
             dealt = w1_bf[g][:].rearrange("p (t m j) -> p m j t", t=PACK, j=PACK)
             raw = w1_raw[g][:].rearrange("p j (m t) -> p m j t", t=PACK)
-            nc.scalar.activation(dealt, raw, ACT.Copy)
+            on_scalar = P if g == 0 else CAST_ON_SCALAR
+            nc.scalar.activation(dealt[:, :on_scalar], raw[:, :on_scalar], ACT.Copy)
+            if on_scalar < P:
+                nc.vector.tensor_copy(dealt[:, on_scalar:], raw[:, on_scalar:])
 
         def quantize_w1(g):
             nc.vector.quantize_mx(out=w1_codes[g][:].bitcast(FP8X4), scales=w1_scale[g][:], in_=w1_bf[g][:])
@@ -166,6 +169,7 @@ def tile_picked_prelu8_none_po_kernel(
             )
 
         above = {}
+        acc = {}
         below = {}
         z = [sbuf([P, CH * PACK], BF16, "z%d" % c) for c in range(NCH)]
         res = [sbuf([P, PACK, CH], F32, "res%d" % c) for c in range(NCH)]
@@ -203,11 +207,11 @@ def tile_picked_prelu8_none_po_kernel(
 
         def second_product(c):
             cols = slice(CH * c, CH * (c + 1))
-            acc = psum.tile([P, PACK, CH], F32, name="acc%d" % c, tag="acc%d" % c)
+            acc[c] = psum.tile([P, PACK, CH], F32, name="acc%d" % c, tag="acc%d" % c)
             for t in range(PACK):
                 dealt_cols = slice(P * t, P * (t + 1))
                 nc.tensor.matmul_mx(
-                    out=acc[:, t, :],
+                    out=acc[c][:, t, :],
                     lhsT=w2_codes[:, dealt_cols].bitcast(FP8X4),
                     lhsT_scale=w2_scale[:, dealt_cols],
                     rhs=z_codes[c][:].bitcast(FP8X4),
@@ -215,16 +219,16 @@ def tile_picked_prelu8_none_po_kernel(
                     start=True,
                     stop=True,
                 )
-            nc.scalar.copy(res[c][:], acc[:])
+            nc.scalar.copy(res[c][:], acc[c][:])
             nc.sync.dma_start(out_rows[:, :, cols], res[c][:])
 
         def round_out(c):
+            runs = ON_SCALAR[c] // RUN
             woven = res_bf[c][:].rearrange("p (r i) t -> p r t i", i=RUN)
-            plain = res[c][:].rearrange("p t (r i) -> p r t i", i=RUN)
-            shared = SHARED_RUNS if c in ROUND_SHARED else 0
-            if shared:
-                nc.scalar.copy(woven[:, :shared], plain[:, :shared])
-            nc.vector.tensor_copy(woven[:, shared:], plain[:, shared:])
+            if runs:
+                nc.scalar.copy(woven[:, :runs], acc[c][:].rearrange("p t (r i) -> p r t i", i=RUN)[:, :runs])
+            if runs < CH // RUN:
+                nc.vector.tensor_copy(woven[:, runs:], res[c][:].rearrange("p t (r i) -> p r t i", i=RUN)[:, runs:])
 
         def quantize_out(c):
             cols = slice(CH * c, CH * (c + 1))
@@ -267,9 +271,9 @@ def tile_picked_prelu8_none_po_kernel(
         join_signs(3)
         quantize_z(2)
         quantize_z(3)
+        round_out(0)
         second_product(2)
         second_product(3)
-        round_out(0)
         round_out(1)
         quantize_out(0)
         quantize_out(1)

@@ -21,17 +21,15 @@ PASSES = K // (P * PACK)
 QUADS = 4
 QUAD = P // QUADS
 ROWS = 4
-SPREAD = QUAD // ROWS
 PLANE = 4
 GROUP = 16
 CH = 128
 NCH = S // CH
+LAST = NCH - 1
 HALF = S // 2
 RUN = 4
-XSTEP = 4
-RES_TAGS = ["z2", "z3", "resbf2", "resbf3"]
-ON_SCALAR = (64, 0, 0, 80)
 CAST_ON_SCALAR = 96
+ROUND_ON_SCALAR = (0, 64, 64, 80)
 
 
 def tile_picked_prelu8_none_po_kernel(
@@ -45,11 +43,25 @@ def tile_picked_prelu8_none_po_kernel(
         def sbuf(shape, dtype, name, takes_over=None):
             return keep.tile(shape, dtype, name=name, tag=takes_over or name, align_bytes=64)
 
+        def half_list(list_sb, h):
+            return list_sb[:, HALF // GROUP * h : HALF // GROUP * (h + 1)]
+
         task_sb = keep.tile([P, S // GROUP], U16, name="task_sb")
         offs_sb = keep.tile([P, S // GROUP], U16, name="offs_sb")
         slope_rows = slope.rearrange("(p t) u -> p t u", t=PACK)
         w1_rows = w1.rearrange("(g p j) c -> g p j c", p=P, j=PACK)
         x_rows = [x_words[g].rearrange("p n t -> p (n t)").bitcast(I32) for g in range(PASSES)]
+
+        w2s_raw = sbuf([P, N], U8, "w2s_raw")
+        nc.gpsimd.memset(w2s_raw[:].bitcast(I32), 0)
+        for r in range(ROWS):
+            nc.gpsimd.dma_start(
+                w2s_raw[r:P:QUAD, :].bitcast(I32), w2_scales[0].rearrange("(q r) n -> r q n", r=ROWS)[r].bitcast(I32)
+            )
+        w2_scale = sbuf([P, N], U8, "w2_scale")
+        nc.gpsimd.tensor_copy(
+            w2_scale[:].rearrange("p (t m) -> p t m", t=PACK), w2s_raw[:].rearrange("p (m t) -> p t m", t=PACK)
+        )
 
         xs_all = sbuf([P, T], U8, "xs_all")
         xs_spread = sbuf([P, S], U8, "xs_spread")
@@ -60,12 +72,9 @@ def tile_picked_prelu8_none_po_kernel(
 
         early_slopes = sbuf([P, (PACK - 1) * U], F32, "early_slopes")
         w1_raw = [sbuf([P, PACK, H], F32, "w1raw%d" % g) for g in range(PASSES)]
-
         x_all = [sbuf([P, T], U32, "x_all0")]
         nc.sync.dma_start(early_slopes[:], slope.rearrange("(p t) u -> p (t u)", t=PACK)[:, : (PACK - 1) * U])
-        nc.sync.dma_start(
-            xs_all[:QUAD, :].bitcast(I32), x_scales.rearrange("g b n -> b g n").bitcast(I32)
-        )
+        nc.sync.dma_start(xs_all[:QUAD, :].bitcast(I32), x_scales.rearrange("g b n -> b g n").bitcast(I32))
         nc.sync.dma_start(offs_sb[:], offs)
         nc.sync.dma_start(task_sb[:], task)
         nc.sync.dma_start(w1_raw[0][:], w1_rows[0])
@@ -76,41 +85,31 @@ def tile_picked_prelu8_none_po_kernel(
             slope_sb.append(sbuf([P, U], F32, "slope%d" % t))
             nc.scalar.copy(slope_sb[t][:], early_slopes[:, U * t : U * (t + 1)])
 
-        def half_list(list_sb, h):
-            return list_sb[:, HALF // GROUP * h : HALF // GROUP * (h + 1)]
-
         low_slope = sbuf([P, 2, S], F32, "low_slope")
         high_slope = [sbuf([P, 2, CH], F32, "high_slope%d" % c) for c in range(NCH)]
 
-        def pick_slopes(t):
-            if t == 0:
-                nc.vector.tensor_copy(low_slope[:, 0, :], early_slopes[:].indirect(task_sb[:]))
-            elif t == 1:
-                for h in range(S // HALF):
-                    nc.vector.tensor_copy(
-                        low_slope[:, t, HALF * h : HALF * (h + 1)], slope_sb[t][:].indirect(half_list(task_sb, h))
-                    )
-            else:
-                for c in range(NCH):
-                    window = slope_sb[t][:].indirect(task_sb[:, CH // GROUP * c : CH // GROUP * (c + 1)])
-                    if t == PACK - 1:
-                        nc.scalar.activation(high_slope[c][:, 1, :], window, ACT.Copy)
-                    else:
-                        nc.vector.tensor_copy(high_slope[c][:, 0, :], window)
+        def chunk_list(list_sb, c):
+            return list_sb[:, CH // GROUP * c : CH // GROUP * (c + 1)]
 
         nc.vector.tensor_copy(xs_spread[:], xs_all[:].indirect(offs_sb[:]))
         for q in range(QUADS):
             nc.scalar.dma_start(
-                xs_picked[QUAD * q + PLANE : QUAD * q + PLANE + ROWS, :].bitcast(I32).rearrange("p (g n) -> p g n", g=PASSES),
+                xs_picked[QUAD * q + PLANE : QUAD * q + PLANE + ROWS, :]
+                .bitcast(I32)
+                .rearrange("p (g n) -> p g n", g=PASSES),
                 xs_spread[PASSES * ROWS * q : PASSES * ROWS * (q + 1), :].bitcast(I32),
             )
-        pick_slopes(0)
+        nc.vector.tensor_copy(low_slope[:, 0, :], early_slopes[:].indirect(task_sb[:]))
         x_all.append(sbuf([P, T], U32, "x_all1", "early_slopes"))
         nc.sync.dma_start(x_all[1][:].bitcast(I32), x_rows[1])
-        pick_slopes(1)
+        for h in range(S // HALF):
+            nc.vector.tensor_copy(
+                low_slope[:, 1, HALF * h : HALF * (h + 1)], slope_sb[1][:].indirect(half_list(task_sb, h))
+            )
         slope_sb.append(sbuf([P, U], F32, "slope3", "slope1"))
         nc.sync.dma_start(slope_sb[3][:], slope_rows[:, 3, :])
-        pick_slopes(2)
+        for c in range(NCH):
+            nc.vector.tensor_copy(high_slope[c][:, 0, :], slope_sb[2][:].indirect(chunk_list(task_sb, c)))
 
         w1_codes = [sbuf([P, H], U32, "w1codes0")]
         w1_scale = [sbuf([P, H], U8, "w1scale%d" % g) for g in range(PASSES)]
@@ -127,15 +126,9 @@ def tile_picked_prelu8_none_po_kernel(
             nc.vector.quantize_mx(out=w1_codes[g][:].bitcast(FP8X4), scales=w1_scale[g][:], in_=w1_bf[g][:])
 
         quantize_w1(0)
-
         w2_raw = sbuf([P, N], I32, "w2_raw", "w1raw0")
         nc.sync.dma_start(w2_raw[:], w2_words[0].rearrange("p n t -> p (n t)").bitcast(I32))
-        w2s_raw = sbuf([P, N], U8, "w2s_raw", "w1bf0")
-        nc.vector.memset(w2s_raw[:].bitcast(I32), 0)
-        for r in range(ROWS):
-            nc.sync.dma_start(
-                w2s_raw[r:P:QUAD, :].bitcast(I32), w2_scales[0].rearrange("(q r) n -> r q n", r=ROWS)[r].bitcast(I32)
-            )
+
         x_picked = [sbuf([P, S], U32, "xpicked%d" % g) for g in range(PASSES)]
         cuts = [[0, HALF, S], [0, CH, HALF, S]]
         for g in range(PASSES):
@@ -144,60 +137,66 @@ def tile_picked_prelu8_none_po_kernel(
             if g == 0:
                 w1_codes.append(sbuf([P, H], U32, "w1codes1", "x_all0"))
                 quantize_w1(1)
-        pick_slopes(3)
+
+        def pick_late(c):
+            nc.scalar.activation(high_slope[c][:, 1, :], slope_sb[3][:].indirect(chunk_list(task_sb, c)), ACT.Copy)
+
+        pick_late(0)
+        pick_late(1)
 
         out_codes = sbuf([P, S], U32, "out_codes")
         out_scale = sbuf([P, S], U8, "out_scale")
         out_rows = out_0.rearrange("(p t) s -> p t s", t=PACK)
         words_out = out_1[0].rearrange("p n t -> p (n t)").bitcast(I32)
 
-        y = [psum.tile([P, PACK, CH], F32, name="y%d" % c, tag="y%d" % c) for c in range(NCH)]
+        banks = ["bank%d" % b for b in range(2 * NCH)]
+        y = [
+            [psum.tile([P, 2, CH], F32, name="y%d_%d" % (c, u), tag=banks[2 * c + u]) for u in range(2)]
+            for c in range(NCH)
+        ]
+        acc = {}
         z_codes = [sbuf([P, CH], U32, "zcodes%d" % c) for c in range(NCH)]
         z_scale = [sbuf([P, CH], U8, "zscale%d" % c) for c in range(NCH)]
-
-        def first_product(c, t, g, first, last):
-            cols = slice(CH * c, CH * (c + 1))
-            feats = slice(P * t, P * (t + 1))
-            nc.tensor.matmul_mx(
-                out=y[c][:, t, :],
-                lhsT=w1_codes[g][:, feats].bitcast(FP8X4),
-                lhsT_scale=w1_scale[g][:, feats],
-                rhs=x_picked[g][:, cols].bitcast(FP8X4),
-                rhs_scale=xs_picked[PLANE:P, S * g + CH * c : S * g + CH * (c + 1)],
-                start=(g == first and t == 0),
-                stop=(g == last and t == PACK - 1),
-            )
-
-        above = {}
-        acc = {}
-        below = {}
         z = [sbuf([P, CH * PACK], BF16, "z%d" % c) for c in range(NCH)]
         res = [sbuf([P, PACK, CH], F32, "res%d" % c) for c in range(NCH)]
-        LAST = NCH - 1
-        res_tags = RES_TAGS
-        res_bf = [sbuf([P, CH, PACK], BF16, "resbf%d" % c, res_tags[c]) for c in range(NCH)]
+        above = {}
+        below = {}
+        res_bf = {}
 
-        def keep_above(c, takes_over=None):
-            above[c] = sbuf([P, CH, PACK], BF16, "above%d" % c, takes_over)
-            nc.scalar.activation(above[c][:], y[c][:].rearrange("p t n -> p n t"), ACT.Relu)
+        def first_product(c, t, g, first, last):
+            feats = slice(P * t, P * (t + 1))
+            nc.tensor.matmul_mx(
+                out=y[c][t // 2][:, t % 2, :],
+                lhsT=w1_codes[g][:, feats].bitcast(FP8X4),
+                lhsT_scale=w1_scale[g][:, feats],
+                rhs=x_picked[g][:, CH * c : CH * (c + 1)].bitcast(FP8X4),
+                rhs_scale=xs_picked[PLANE:P, S * g + CH * c : S * g + CH * (c + 1)],
+                start=(g == first and t % 2 == 0),
+                stop=(g == last and t % 2 == 1),
+            )
 
-        def scale_below(c, takes_over=None):
-            below[c] = sbuf([P, 2, CH, 2], BF16, "below%d" % c, takes_over)
-            pairs = [low_slope[:, :, CH * c : CH * (c + 1)], high_slope[c][:]]
-            for u in range(2):
-                nc.vector.scalar_tensor_tensor(
-                    below[c][:, u],
-                    y[c][:, 2 * u : 2 * u + 2, :].rearrange("p e n -> p n e"),
-                    0.0,
-                    pairs[u].rearrange("p e n -> p n e"),
-                    ALU.min,
-                    ALU.mult,
-                )
+        def keep_above(c, u, takes_over=None):
+            if c not in above:
+                above[c] = sbuf([P, 2, CH, 2], BF16, "above%d" % c, takes_over)
+            nc.scalar.activation(above[c][:, u], y[c][u][:].rearrange("p e n -> p n e"), ACT.Relu)
+
+        def scale_below(c, u, takes_over=None):
+            if c not in below:
+                below[c] = sbuf([P, 2, CH, 2], BF16, "below%d" % c, takes_over)
+            slopes = low_slope[:, :, CH * c : CH * (c + 1)] if u == 0 else high_slope[c][:]
+            nc.vector.scalar_tensor_tensor(
+                below[c][:, u],
+                y[c][u][:].rearrange("p e n -> p n e"),
+                0.0,
+                slopes.rearrange("p e n -> p n e"),
+                ALU.min,
+                ALU.mult,
+            )
 
         def join_signs(c):
             nc.vector.tensor_tensor(
                 z[c][:].rearrange("p (n u e) -> p n u e", u=2, e=2),
-                above[c][:].rearrange("p n (u e) -> p n u e", u=2),
+                above[c][:].rearrange("p u n e -> p n u e"),
                 below[c][:].rearrange("p u n e -> p n u e"),
                 ALU.add,
             )
@@ -206,8 +205,7 @@ def tile_picked_prelu8_none_po_kernel(
             nc.vector.quantize_mx(out=z_codes[c][:].bitcast(FP8X4), scales=z_scale[c][:], in_=z[c][:])
 
         def second_product(c):
-            cols = slice(CH * c, CH * (c + 1))
-            acc[c] = psum.tile([P, PACK, CH], F32, name="acc%d" % c, tag="acc%d" % c)
+            acc[c] = psum.tile([P, PACK, CH], F32, name="acc%d" % c, tag=banks[c])
             for t in range(PACK):
                 dealt_cols = slice(P * t, P * (t + 1))
                 nc.tensor.matmul_mx(
@@ -219,11 +217,14 @@ def tile_picked_prelu8_none_po_kernel(
                     start=True,
                     stop=True,
                 )
-            nc.scalar.copy(res[c][:], acc[c][:])
-            nc.sync.dma_start(out_rows[:, :, cols], res[c][:])
 
-        def round_out(c):
-            runs = ON_SCALAR[c] // RUN
+        def store_result(c):
+            nc.scalar.copy(res[c][:], acc[c][:])
+            nc.sync.dma_start(out_rows[:, :, CH * c : CH * (c + 1)], res[c][:])
+
+        def round_out(c, takes_over=None):
+            res_bf[c] = sbuf([P, CH, PACK], BF16, "resbf%d" % c, takes_over)
+            runs = ROUND_ON_SCALAR[c] // RUN
             woven = res_bf[c][:].rearrange("p (r i) t -> p r t i", i=RUN)
             if runs:
                 nc.scalar.copy(woven[:, :runs], acc[c][:].rearrange("p t (r i) -> p r t i", i=RUN)[:, :runs])
@@ -238,6 +239,10 @@ def tile_picked_prelu8_none_po_kernel(
                 in_=res_bf[c][:].rearrange("p n t -> p (n t)"),
             )
 
+        def store_words(h):
+            cols = slice(HALF * h, HALF * (h + 1))
+            nc.sync.dma_start(words_out[:, cols], out_codes[:, cols].bitcast(I32))
+
         for g in range(PASSES):
             for c in range(LAST):
                 for t in range(PACK):
@@ -249,39 +254,50 @@ def tile_picked_prelu8_none_po_kernel(
         nc.gpsimd.tensor_copy(
             w2_codes[:].rearrange("p (t m) -> p t m", t=PACK), w2_raw[:].rearrange("p (m t) -> p t m", t=PACK)
         )
-        w2_scale = sbuf([P, N], U8, "w2_scale", "w1raw0")
-        nc.gpsimd.tensor_copy(
-            w2_scale[:].rearrange("p (t m) -> p t m", t=PACK), w2s_raw[:].rearrange("p (m t) -> p t m", t=PACK)
-        )
-        scale_below(0)
-        keep_above(0)
-        scale_below(1)
-        keep_above(1)
-        scale_below(2, "high_slope0")
-        keep_above(3, "high_slope1")
+        scale_below(0, 0)
+        keep_above(0, 1)
+        scale_below(1, 0)
+        keep_above(1, 1)
+        keep_above(0, 0)
+        scale_below(0, 1)
+        keep_above(1, 0)
+        scale_below(1, 1)
         join_signs(0)
-        join_signs(1)
-        keep_above(2, "above1")
+        pick_late(2)
+        pick_late(3)
+        scale_below(2, 0, "high_slope1")
         quantize_z(0)
+        keep_above(2, 1, "above0")
+        keep_above(2, 0)
+        keep_above(3, 1, "below0")
+        join_signs(1)
+        scale_below(2, 1)
         quantize_z(1)
+        scale_below(3, 0, "below1")
         second_product(0)
-        second_product(1)
-        scale_below(3, "below1")
+        store_result(0)
+        keep_above(3, 0)
         join_signs(2)
-        join_signs(3)
+        scale_below(3, 1)
         quantize_z(2)
-        quantize_z(3)
+        second_product(1)
+        store_result(1)
+        join_signs(3)
         round_out(0)
-        second_product(2)
-        second_product(3)
+        quantize_z(3)
         round_out(1)
+        second_product(2)
+        store_result(2)
         quantize_out(0)
         quantize_out(1)
+        store_words(0)
         round_out(2)
-        round_out(3)
+        second_product(3)
+        store_result(3)
         quantize_out(2)
+        round_out(3)
         quantize_out(3)
-        nc.sync.dma_start(words_out, out_codes[:].bitcast(I32))
+        store_words(1)
         for r in range(ROWS):
             queue = nc.scalar if r % 2 == 0 else nc.sync
             queue.dma_start(

@@ -28,8 +28,8 @@ NCH = S // CH
 LAST = NCH - 1
 HALF = S // 2
 RUN = 4
-CAST_ON_SCALAR = 96
-ROUND_ON_SCALAR = (0, 64, 64, 80)
+CAST_ON_SCALAR = 48
+ROUND_ON_SCALAR = (32, 128, 64, 80)
 
 
 def tile_picked_prelu8_none_po_kernel(
@@ -71,14 +71,13 @@ def tile_picked_prelu8_none_po_kernel(
         nc.vector.memset(xs_picked[:].bitcast(I32), 0)
 
         early_slopes = sbuf([P, (PACK - 1) * U], F32, "early_slopes")
-        w1_raw = [sbuf([P, PACK, H], F32, "w1raw%d" % g) for g in range(PASSES)]
+        w1_raw = [sbuf([P, PACK, H], F32, "w1raw0")]
         x_all = [sbuf([P, T], U32, "x_all0")]
         nc.sync.dma_start(early_slopes[:], slope.rearrange("(p t) u -> p (t u)", t=PACK)[:, : (PACK - 1) * U])
         nc.sync.dma_start(xs_all[:QUAD, :].bitcast(I32), x_scales.rearrange("g b n -> b g n").bitcast(I32))
         nc.sync.dma_start(offs_sb[:], offs)
         nc.sync.dma_start(task_sb[:], task)
         nc.sync.dma_start(w1_raw[0][:], w1_rows[0])
-        nc.sync.dma_start(w1_raw[1][:], w1_rows[1])
         nc.sync.dma_start(x_all[0][:].bitcast(I32), x_rows[0])
         slope_sb = [early_slopes]
         for t in range(1, PACK - 1):
@@ -99,6 +98,8 @@ def tile_picked_prelu8_none_po_kernel(
                 .rearrange("p (g n) -> p g n", g=PASSES),
                 xs_spread[PASSES * ROWS * q : PASSES * ROWS * (q + 1), :].bitcast(I32),
             )
+        w1_raw.append(sbuf([P, PACK, H], F32, "w1raw1", "xs_all"))
+        nc.sync.dma_start(w1_raw[1][:], w1_rows[1])
         nc.vector.tensor_copy(low_slope[:, 0, :], early_slopes[:].indirect(task_sb[:]))
         x_all.append(sbuf([P, T], U32, "x_all1", "early_slopes"))
         nc.sync.dma_start(x_all[1][:].bitcast(I32), x_rows[1])
@@ -114,7 +115,8 @@ def tile_picked_prelu8_none_po_kernel(
         w1_codes = [sbuf([P, H], U32, "w1codes0")]
         w1_scale = [sbuf([P, H], U8, "w1scale%d" % g) for g in range(PASSES)]
         w1_bf = [sbuf([P, H * PACK], BF16, "w1bf%d" % g) for g in range(PASSES)]
-        for g in range(PASSES):
+
+        def cast_w1(g):
             dealt = w1_bf[g][:].rearrange("p (t m j) -> p m j t", t=PACK, j=PACK)
             raw = w1_raw[g][:].rearrange("p j (m t) -> p m j t", t=PACK)
             on_scalar = P if g == 0 else CAST_ON_SCALAR
@@ -125,6 +127,7 @@ def tile_picked_prelu8_none_po_kernel(
         def quantize_w1(g):
             nc.vector.quantize_mx(out=w1_codes[g][:].bitcast(FP8X4), scales=w1_scale[g][:], in_=w1_bf[g][:])
 
+        cast_w1(0)
         quantize_w1(0)
         w2_raw = sbuf([P, N], I32, "w2_raw", "w1raw0")
         nc.sync.dma_start(w2_raw[:], w2_words[0].rearrange("p n t -> p (n t)").bitcast(I32))
@@ -135,7 +138,8 @@ def tile_picked_prelu8_none_po_kernel(
             for a, b in zip(cuts[g], cuts[g][1:]):
                 nc.vector.tensor_copy(x_picked[g][:, a:b], x_all[g][:].indirect(offs_sb[:, a // GROUP : b // GROUP]))
             if g == 0:
-                w1_codes.append(sbuf([P, H], U32, "w1codes1", "x_all0"))
+                cast_w1(1)
+                w1_codes.append(sbuf([P, H], U32, "w1codes1"))
                 quantize_w1(1)
 
         def pick_late(c):
@@ -250,7 +254,7 @@ def tile_picked_prelu8_none_po_kernel(
         for g in (1, 0):
             for t in range(PACK):
                 first_product(LAST, t, g, 1, 0)
-        w2_codes = sbuf([P, N], I32, "w2_codes", "early_slopes")
+        w2_codes = sbuf([P, N], I32, "w2_codes")
         nc.gpsimd.tensor_copy(
             w2_codes[:].rearrange("p (t m) -> p t m", t=PACK), w2_raw[:].rearrange("p (m t) -> p t m", t=PACK)
         )

@@ -29,7 +29,9 @@ LAST = NCH - 1
 HALF = S // 2
 RUN = 4
 CAST_ON_SCALAR = 48
-ROUND_ON_SCALAR = (32, 128, 64, 80)
+MID = CH // 2
+FIRST_SPLIT = 32
+RES_TAGS = ["resbf0", "resbf1", "resbf2", "resbf3"]
 
 
 def tile_picked_prelu8_none_po_kernel(
@@ -165,7 +167,7 @@ def tile_picked_prelu8_none_po_kernel(
         res = [sbuf([P, PACK, CH], F32, "res%d" % c) for c in range(NCH)]
         above = {}
         below = {}
-        res_bf = {}
+        res_bf = [sbuf([P, CH, PACK], BF16, "resbf%d" % c, RES_TAGS[c]) for c in range(NCH)]
 
         def first_product(c, t, g, first, last):
             feats = slice(P * t, P * (t + 1))
@@ -197,43 +199,47 @@ def tile_picked_prelu8_none_po_kernel(
                 ALU.mult,
             )
 
-        def join_signs(c):
+        def join_signs(c, a=0, b=CH):
             nc.vector.tensor_tensor(
-                z[c][:].rearrange("p (n u e) -> p n u e", u=2, e=2),
-                above[c][:].rearrange("p u n e -> p n u e"),
-                below[c][:].rearrange("p u n e -> p n u e"),
+                z[c][:].rearrange("p (n u e) -> p n u e", u=2, e=2)[:, a:b],
+                above[c][:].rearrange("p u n e -> p n u e")[:, a:b],
+                below[c][:].rearrange("p u n e -> p n u e")[:, a:b],
                 ALU.add,
             )
 
-        def quantize_z(c):
-            nc.vector.quantize_mx(out=z_codes[c][:].bitcast(FP8X4), scales=z_scale[c][:], in_=z[c][:])
+        def quantize_z(c, a=0, b=CH):
+            nc.vector.quantize_mx(
+                out=z_codes[c][:, a:b].bitcast(FP8X4), scales=z_scale[c][:, a:b], in_=z[c][:, PACK * a : PACK * b]
+            )
 
-        def second_product(c):
-            acc[c] = psum.tile([P, PACK, CH], F32, name="acc%d" % c, tag=banks[c])
+        def second_product(c, bank, a=0, b=CH):
+            acc[bank] = psum.tile([P, PACK, b - a], F32, name="acc%d" % bank, tag=banks[bank])
             for t in range(PACK):
                 dealt_cols = slice(P * t, P * (t + 1))
                 nc.tensor.matmul_mx(
-                    out=acc[c][:, t, :],
+                    out=acc[bank][:, t, :],
                     lhsT=w2_codes[:, dealt_cols].bitcast(FP8X4),
                     lhsT_scale=w2_scale[:, dealt_cols],
-                    rhs=z_codes[c][:].bitcast(FP8X4),
-                    rhs_scale=z_scale[c][:],
+                    rhs=z_codes[c][:, a:b].bitcast(FP8X4),
+                    rhs_scale=z_scale[c][:, a:b],
                     start=True,
                     stop=True,
                 )
+            nc.scalar.copy(res[c][:, :, a:b], acc[bank][:])
 
         def store_result(c):
-            nc.scalar.copy(res[c][:], acc[c][:])
             nc.sync.dma_start(out_rows[:, :, CH * c : CH * (c + 1)], res[c][:])
 
-        def round_out(c, takes_over=None):
-            res_bf[c] = sbuf([P, CH, PACK], BF16, "resbf%d" % c, takes_over)
-            runs = ROUND_ON_SCALAR[c] // RUN
-            woven = res_bf[c][:].rearrange("p (r i) t -> p r t i", i=RUN)
-            if runs:
-                nc.scalar.copy(woven[:, :runs], acc[c][:].rearrange("p t (r i) -> p r t i", i=RUN)[:, :runs])
-            if runs < CH // RUN:
-                nc.vector.tensor_copy(woven[:, runs:], res[c][:].rearrange("p t (r i) -> p r t i", i=RUN)[:, runs:])
+        def woven(c, a, b):
+            return res_bf[c][:].rearrange("p (r i) t -> p r t i", i=RUN)[:, a // RUN : b // RUN]
+
+        def round_from_bank(c, a, b, bank, first=0):
+            runs = acc[bank][:].rearrange("p t (r i) -> p r t i", i=RUN)
+            nc.scalar.copy(woven(c, a, b), runs[:, (a - first) // RUN : (b - first) // RUN])
+
+        def round_from_copy(c, a, b):
+            runs = res[c][:].rearrange("p t (r i) -> p r t i", i=RUN)
+            nc.vector.tensor_copy(woven(c, a, b), runs[:, a // RUN : b // RUN])
 
         def quantize_out(c):
             cols = slice(CH * c, CH * (c + 1))
@@ -278,28 +284,33 @@ def tile_picked_prelu8_none_po_kernel(
         scale_below(2, 1)
         quantize_z(1)
         scale_below(3, 0, "below1")
-        second_product(0)
+        second_product(0, 0)
         store_result(0)
         keep_above(3, 0)
+        round_from_bank(0, 0, FIRST_SPLIT, 0)
         join_signs(2)
         scale_below(3, 1)
         quantize_z(2)
-        second_product(1)
+        second_product(1, 1)
         store_result(1)
-        join_signs(3)
-        round_out(0)
-        quantize_z(3)
-        round_out(1)
-        second_product(2)
+        join_signs(3, 0, MID)
+        join_signs(3, MID, CH)
+        quantize_z(3, 0, MID)
+        quantize_z(3, MID, CH)
+        round_from_copy(0, FIRST_SPLIT, CH)
+        round_from_bank(1, 0, CH, 1)
+        second_product(2, 2)
         store_result(2)
-        quantize_out(0)
-        quantize_out(1)
-        store_words(0)
-        round_out(2)
-        second_product(3)
+        second_product(3, 3, 0, MID)
+        second_product(3, 4, MID, CH)
         store_result(3)
+        quantize_out(1)
+        quantize_out(0)
+        store_words(0)
+        round_from_copy(2, 0, CH)
+        round_from_copy(3, 0, MID)
+        round_from_bank(3, MID, CH, 4, MID)
         quantize_out(2)
-        round_out(3)
         quantize_out(3)
         store_words(1)
         for r in range(ROWS):

@@ -158,8 +158,9 @@ def tile_picked_prelu8_none_po_kernel(
         banks = ["bank%d" % b for b in range(2 * NCH)]
         y = [
             [psum.tile([P, 2, CH], F32, name="y%d_%d" % (c, u), tag=banks[2 * c + u]) for u in range(2)]
-            for c in range(NCH)
+            for c in range(LAST)
         ]
+        y.append({})
         acc = {}
         z_codes = [sbuf([P, CH], U32, "zcodes%d" % c) for c in range(NCH)]
         z_scale = [sbuf([P, CH], U8, "zscale%d" % c) for c in range(NCH)]
@@ -241,12 +242,12 @@ def tile_picked_prelu8_none_po_kernel(
             runs = res[c][:].rearrange("p t (r i) -> p r t i", i=RUN)
             nc.vector.tensor_copy(woven(c, a, b), runs[:, a // RUN : b // RUN])
 
-        def quantize_out(c):
-            cols = slice(CH * c, CH * (c + 1))
+        def quantize_out(c, a=0, b=CH):
+            cols = slice(CH * c + a, CH * c + b)
             nc.vector.quantize_mx(
                 out=out_codes[:, cols].bitcast(FP8X4),
                 scales=out_scale[:, cols],
-                in_=res_bf[c][:].rearrange("p n t -> p (n t)"),
+                in_=res_bf[c][:, a:b].rearrange("p n t -> p (n t)"),
             )
 
         def store_words(h):
@@ -257,9 +258,14 @@ def tile_picked_prelu8_none_po_kernel(
             for c in range(LAST):
                 for t in range(PACK):
                     first_product(c, t, g, 0, 1)
-        for g in (1, 0):
-            for t in range(PACK):
-                first_product(LAST, t, g, 1, 0)
+
+        def late_product(u, bank):
+            y[LAST][u] = psum.tile([P, 2, CH], F32, name="y%d_%d" % (LAST, u), tag=banks[bank])
+            for g in (1, 0):
+                for t in (2 * u, 2 * u + 1):
+                    first_product(LAST, t, g, 1, 0)
+
+        late_product(1, 7)
         w2_codes = sbuf([P, N], I32, "w2_codes")
         nc.gpsimd.tensor_copy(
             w2_codes[:].rearrange("p (t m) -> p t m", t=PACK), w2_raw[:].rearrange("p (m t) -> p t m", t=PACK)
@@ -271,6 +277,7 @@ def tile_picked_prelu8_none_po_kernel(
         keep_above(0, 0)
         scale_below(0, 1)
         keep_above(1, 0)
+        late_product(0, 2)
         scale_below(1, 1)
         join_signs(0)
         pick_late(2)
@@ -299,7 +306,7 @@ def tile_picked_prelu8_none_po_kernel(
         quantize_z(3, MID, CH)
         round_from_copy(0, FIRST_SPLIT, CH)
         round_from_bank(1, 0, CH, 1)
-        second_product(2, 2)
+        second_product(2, 6)
         store_result(2)
         second_product(3, 3, 0, MID)
         second_product(3, 4, MID, CH)
@@ -311,7 +318,8 @@ def tile_picked_prelu8_none_po_kernel(
         round_from_copy(3, 0, MID)
         round_from_bank(3, MID, CH, 4, MID)
         quantize_out(2)
-        quantize_out(3)
+        quantize_out(3, 0, MID)
+        quantize_out(3, MID, CH)
         store_words(1)
         for r in range(ROWS):
             queue = nc.scalar if r % 2 == 0 else nc.sync

@@ -43,7 +43,7 @@ def tile_picked_prelu8_none_po_kernel(
         psum = ctx.enter_context(tc.psum_pool(name="psum", bufs=1))
 
         def sbuf(shape, dtype, name, takes_over=None):
-            return keep.tile(shape, dtype, name=name, tag=takes_over or name, align_bytes=64)
+            return keep.tile(shape, dtype, name=name, tag=takes_over or name, align_bytes=256)
 
         def half_list(list_sb, h):
             return list_sb[:, HALF // GROUP * h : HALF // GROUP * (h + 1)]

from contextlib import ExitStack

import concourse.mybir as mybir

K, T, S, H, N, U = 1024, 2048, 512, 512, 512, 512
FLOPS = 2 * K * H * S + 2 * H * N * S

F32 = mybir.dt.float32
BF16 = mybir.dt.bfloat16
I32 = mybir.dt.int32
U32 = mybir.dt.uint32
U16 = mybir.dt.uint16
U8 = mybir.dt.uint8
FP8X4 = mybir.dt.float8_e4m3fn_x4
ALU = mybir.AluOpType
ACT = mybir.ActivationFunctionType

P = 128
PACK = 4
PASSES = K // (P * PACK)
QUADS = 4
QUAD = P // QUADS
ROWS = 4
PLANE = 4
GROUP = 16
CH = 128
NCH = S // CH
LAST = NCH - 1
HALF = S // 2
RUN = 4
CAST_ON_SCALAR = 48
MID = CH // 2
FIRST_SPLIT = 32
RES_TAGS = ["resbf0", "resbf1", "resbf2", "resbf3"]


def tile_picked_prelu8_none_po_kernel(
    tc, x_words, x_scales, w1, slope, w2_words, w2_scales, offs, task, out_0, out_1, out_2
):
    nc = tc.nc
    with ExitStack() as ctx:
        keep = ctx.enter_context(tc.tile_pool(name="keep", bufs=1))
        psum = ctx.enter_context(tc.psum_pool(name="psum", bufs=1))

        def sbuf(shape, dtype, name, takes_over=None):
            return keep.tile(shape, dtype, name=name, tag=takes_over or name, align_bytes=256)

        def half_list(list_sb, h):
            return list_sb[:, HALF // GROUP * h : HALF // GROUP * (h + 1)]

        task_sb = keep.tile([P, S // GROUP], U16, name="task_sb")
        offs_sb = keep.tile([P, S // GROUP], U16, name="offs_sb")
        slope_rows = slope.rearrange("(p t) u -> p t u", t=PACK)
        w1_rows = w1.rearrange("(g p j) c -> g p j c", p=P, j=PACK)
        x_rows = [x_words[g].rearrange("p n t -> p (n t)").bitcast(I32) for g in range(PASSES)]

        w2s_raw = sbuf([P, N], U8, "w2s_raw")
        nc.gpsimd.memset(w2s_raw[:].bitcast(I32), 0)
        for r in range(ROWS):
            nc.gpsimd.dma_start(
                w2s_raw[r:P:QUAD, :].bitcast(I32), w2_scales[0].rearrange("(q r) n -> r q n", r=ROWS)[r].bitcast(I32)
            )
        w2_scale = sbuf([P, N], U8, "w2_scale")
        nc.gpsimd.tensor_copy(
            w2_scale[:].rearrange("p (t m) -> p t m", t=PACK), w2s_raw[:].rearrange("p (m t) -> p t m", t=PACK)
        )

        xs_all = sbuf([P, T], U8, "xs_all")
        xs_spread = sbuf([P, S], U8, "xs_spread")
        xs_picked = sbuf([P, PASSES * S], U8, "xs_picked")
        nc.vector.memset(xs_all[QUAD : 2 * QUAD, :].bitcast(I32), 0)
        nc.vector.memset(xs_all[2 * QUAD :, :].bitcast(I32), 0)
        nc.vector.memset(xs_picked[:].bitcast(I32), 0)

        early_slopes = sbuf([P, (PACK - 1) * U], F32, "early_slopes")
        w1_raw = [sbuf([P, PACK, H], F32, "w1raw0")]
        x_all = [sbuf([P, T], U32, "x_all0")]
        nc.sync.dma_start(early_slopes[:], slope.rearrange("(p t) u -> p (t u)", t=PACK)[:, : (PACK - 1) * U])
        nc.sync.dma_start(xs_all[:QUAD, :].bitcast(I32), x_scales.rearrange("g b n -> b g n").bitcast(I32))
        nc.sync.dma_start(offs_sb[:], offs)
        nc.sync.dma_start(task_sb[:], task)
        nc.sync.dma_start(w1_raw[0][:], w1_rows[0])
        nc.sync.dma_start(x_all[0][:].bitcast(I32), x_rows[0])
        slope_sb = [early_slopes]
        for t in range(1, PACK - 1):
            slope_sb.append(sbuf([P, U], F32, "slope%d" % t))
            nc.scalar.copy(slope_sb[t][:], early_slopes[:, U * t : U * (t + 1)])

        low_slope = sbuf([P, 2, S], F32, "low_slope")
        high_slope = [sbuf([P, 2, CH], F32, "high_slope%d" % c) for c in range(NCH)]

        def chunk_list(list_sb, c):
            return list_sb[:, CH // GROUP * c : CH // GROUP * (c + 1)]

        nc.vector.tensor_copy(xs_spread[:], xs_all[:].indirect(offs_sb[:]))
        for q in range(QUADS):
            nc.scalar.dma_start(
                xs_picked[QUAD * q + PLANE : QUAD * q + PLANE + ROWS, :]
                .bitcast(I32)
                .rearrange("p (g n) -> p g n", g=PASSES),
                xs_spread[PASSES * ROWS * q : PASSES * ROWS * (q + 1), :].bitcast(I32),
            )
        w1_raw.append(sbuf([P, PACK, H], F32, "w1raw1", "xs_all"))
        nc.sync.dma_start(w1_raw[1][:], w1_rows[1])
        nc.vector.tensor_copy(low_slope[:, 0, :], early_slopes[:].indirect(task_sb[:]))
        x_all.append(sbuf([P, T], U32, "x_all1", "early_slopes"))
        nc.sync.dma_start(x_all[1][:].bitcast(I32), x_rows[1])
        for h in range(S // HALF):
            nc.vector.tensor_copy(
                low_slope[:, 1, HALF * h : HALF * (h + 1)], slope_sb[1][:].indirect(half_list(task_sb, h))
            )
        slope_sb.append(sbuf([P, U], F32, "slope3", "slope1"))
        nc.sync.dma_start(slope_sb[3][:], slope_rows[:, 3, :])
        for c in range(NCH):
            nc.vector.tensor_copy(high_slope[c][:, 0, :], slope_sb[2][:].indirect(chunk_list(task_sb, c)))

        w1_codes = [sbuf([P, H], U32, "w1codes0")]
        w1_scale = [sbuf([P, H], U8, "w1scale%d" % g) for g in range(PASSES)]
        w1_bf = [sbuf([P, H * PACK], BF16, "w1bf%d" % g) for g in range(PASSES)]

        def cast_w1(g):
            dealt = w1_bf[g][:].rearrange("p (t m j) -> p m j t", t=PACK, j=PACK)
            raw = w1_raw[g][:].rearrange("p j (m t) -> p m j t", t=PACK)
            on_scalar = P if g == 0 else CAST_ON_SCALAR
            nc.scalar.activation(dealt[:, :on_scalar], raw[:, :on_scalar], ACT.Copy)
            if on_scalar < P:
                nc.vector.tensor_copy(dealt[:, on_scalar:], raw[:, on_scalar:])

        def quantize_w1(g):
            nc.vector.quantize_mx(out=w1_codes[g][:].bitcast(FP8X4), scales=w1_scale[g][:], in_=w1_bf[g][:])

        cast_w1(0)
        quantize_w1(0)
        w2_raw = sbuf([P, N], I32, "w2_raw", "w1raw0")
        nc.sync.dma_start(w2_raw[:], w2_words[0].rearrange("p n t -> p (n t)").bitcast(I32))

        x_picked = [sbuf([P, S], U32, "xpicked%d" % g) for g in range(PASSES)]
        cuts = [[0, HALF, S], [0, CH, HALF, S]]
        for g in range(PASSES):
            for a, b in zip(cuts[g], cuts[g][1:]):
                nc.vector.tensor_copy(x_picked[g][:, a:b], x_all[g][:].indirect(offs_sb[:, a // GROUP : b // GROUP]))
            if g == 0:
                cast_w1(1)
                w1_codes.append(sbuf([P, H], U32, "w1codes1"))
                quantize_w1(1)

        def pick_late(c):
            nc.scalar.activation(high_slope[c][:, 1, :], slope_sb[3][:].indirect(chunk_list(task_sb, c)), ACT.Copy)

        pick_late(0)
        pick_late(1)

        out_codes = sbuf([P, S], U32, "out_codes")
        out_scale = sbuf([P, S], U8, "out_scale")
        out_rows = out_0.rearrange("(p t) s -> p t s", t=PACK)
        words_out = out_1[0].rearrange("p n t -> p (n t)").bitcast(I32)

        banks = ["bank%d" % b for b in range(2 * NCH)]
        y = [
            [psum.tile([P, 2, CH], F32, name="y%d_%d" % (c, u), tag=banks[2 * c + u]) for u in range(2)]
            for c in range(LAST)
        ]
        y.append({})
        acc = {}
        z_codes = [sbuf([P, CH], U32, "zcodes%d" % c) for c in range(NCH)]
        z_scale = [sbuf([P, CH], U8, "zscale%d" % c) for c in range(NCH)]
        z = [sbuf([P, CH * PACK], BF16, "z%d" % c) for c in range(NCH)]
        res = [sbuf([P, PACK, CH], F32, "res%d" % c) for c in range(NCH)]
        above = {}
        below = {}
        res_bf = [sbuf([P, CH, PACK], BF16, "resbf%d" % c, RES_TAGS[c]) for c in range(NCH)]

        def first_product(c, t, g, first, last):
            feats = slice(P * t, P * (t + 1))
            nc.tensor.matmul_mx(
                out=y[c][t // 2][:, t % 2, :],
                lhsT=w1_codes[g][:, feats].bitcast(FP8X4),
                lhsT_scale=w1_scale[g][:, feats],
                rhs=x_picked[g][:, CH * c : CH * (c + 1)].bitcast(FP8X4),
                rhs_scale=xs_picked[PLANE:P, S * g + CH * c : S * g + CH * (c + 1)],
                start=(g == first and t % 2 == 0),
                stop=(g == last and t % 2 == 1),
            )

        def keep_above(c, u, takes_over=None):
            if c not in above:
                above[c] = sbuf([P, 2, CH, 2], BF16, "above%d" % c, takes_over)
            nc.scalar.activation(above[c][:, u], y[c][u][:].rearrange("p e n -> p n e"), ACT.Relu)

        def scale_below(c, u, takes_over=None):
            if c not in below:
                below[c] = sbuf([P, 2, CH, 2], BF16, "below%d" % c, takes_over)
            slopes = low_slope[:, :, CH * c : CH * (c + 1)] if u == 0 else high_slope[c][:]
            nc.vector.scalar_tensor_tensor(
                below[c][:, u],
                y[c][u][:].rearrange("p e n -> p n e"),
                0.0,
                slopes.rearrange("p e n -> p n e"),
                ALU.min,
                ALU.mult,
            )

        def join_signs(c, a=0, b=CH):
            nc.vector.tensor_tensor(
                z[c][:].rearrange("p (n u e) -> p n u e", u=2, e=2)[:, a:b],
                above[c][:].rearrange("p u n e -> p n u e")[:, a:b],
                below[c][:].rearrange("p u n e -> p n u e")[:, a:b],
                ALU.add,
            )

        def quantize_z(c, a=0, b=CH):
            nc.vector.quantize_mx(
                out=z_codes[c][:, a:b].bitcast(FP8X4), scales=z_scale[c][:, a:b], in_=z[c][:, PACK * a : PACK * b]
            )

        def second_product(c, bank, a=0, b=CH):
            acc[bank] = psum.tile([P, PACK, b - a], F32, name="acc%d" % bank, tag=banks[bank])
            for t in range(PACK):
                dealt_cols = slice(P * t, P * (t + 1))
                nc.tensor.matmul_mx(
                    out=acc[bank][:, t, :],
                    lhsT=w2_codes[:, dealt_cols].bitcast(FP8X4),
                    lhsT_scale=w2_scale[:, dealt_cols],
                    rhs=z_codes[c][:, a:b].bitcast(FP8X4),
                    rhs_scale=z_scale[c][:, a:b],
                    start=True,
                    stop=True,
                )
            nc.scalar.copy(res[c][:, :, a:b], acc[bank][:])

        def store_result(c):
            nc.sync.dma_start(out_rows[:, :, CH * c : CH * (c + 1)], res[c][:])

        def woven(c, a, b):
            return res_bf[c][:].rearrange("p (r i) t -> p r t i", i=RUN)[:, a // RUN : b // RUN]

        def round_from_bank(c, a, b, bank, first=0):
            runs = acc[bank][:].rearrange("p t (r i) -> p r t i", i=RUN)
            nc.scalar.copy(woven(c, a, b), runs[:, (a - first) // RUN : (b - first) // RUN])

        def round_from_copy(c, a, b):
            runs = res[c][:].rearrange("p t (r i) -> p r t i", i=RUN)
            nc.vector.tensor_copy(woven(c, a, b), runs[:, a // RUN : b // RUN])

        def quantize_out(c, a=0, b=CH):
            cols = slice(CH * c + a, CH * c + b)
            nc.vector.quantize_mx(
                out=out_codes[:, cols].bitcast(FP8X4),
                scales=out_scale[:, cols],
                in_=res_bf[c][:, a:b].rearrange("p n t -> p (n t)"),
            )

        def store_words(h):
            cols = slice(HALF * h, HALF * (h + 1))
            nc.sync.dma_start(words_out[:, cols], out_codes[:, cols].bitcast(I32))

        for g in range(PASSES):
            for c in range(LAST):
                for t in range(PACK):
                    first_product(c, t, g, 0, 1)

        def late_product(u, bank):
            y[LAST][u] = psum.tile([P, 2, CH], F32, name="y%d_%d" % (LAST, u), tag=banks[bank])
            for g in (1, 0):
                for t in (2 * u, 2 * u + 1):
                    first_product(LAST, t, g, 1, 0)

        late_product(1, 7)
        w2_codes = sbuf([P, N], I32, "w2_codes")
        nc.gpsimd.tensor_copy(
            w2_codes[:].rearrange("p (t m) -> p t m", t=PACK), w2_raw[:].rearrange("p (m t) -> p t m", t=PACK)
        )
        scale_below(0, 0)
        keep_above(0, 1)
        scale_below(1, 0)
        keep_above(1, 1)
        keep_above(0, 0)
        scale_below(0, 1)
        keep_above(1, 0)
        late_product(0, 2)
        scale_below(1, 1)
        join_signs(0)
        pick_late(2)
        pick_late(3)
        scale_below(2, 0, "high_slope1")
        quantize_z(0)
        keep_above(2, 1, "above0")
        keep_above(2, 0)
        keep_above(3, 1, "below0")
        join_signs(1)
        scale_below(2, 1)
        quantize_z(1)
        scale_below(3, 0, "below1")
        second_product(0, 0)
        store_result(0)
        keep_above(3, 0)
        round_from_bank(0, 0, FIRST_SPLIT, 0)
        join_signs(2)
        scale_below(3, 1)
        quantize_z(2)
        second_product(1, 1)
        store_result(1)
        join_signs(3, 0, MID)
        join_signs(3, MID, CH)
        quantize_z(3, 0, MID)
        quantize_z(3, MID, CH)
        round_from_copy(0, FIRST_SPLIT, CH)
        round_from_bank(1, 0, CH, 1)
        second_product(2, 6)
        store_result(2)
        second_product(3, 3, 0, MID)
        second_product(3, 4, MID, CH)
        store_result(3)
        quantize_out(1)
        quantize_out(0)
        store_words(0)
        round_from_copy(2, 0, CH)
        round_from_copy(3, 0, MID)
        round_from_bank(3, MID, CH, 4, MID)
        quantize_out(2)
        quantize_out(3, 0, MID)
        quantize_out(3, MID, CH)
        store_words(1)
        for r in range(ROWS):
            queue = nc.scalar if r % 2 == 0 else nc.sync
            queue.dma_start(
                out_2[0].rearrange("(q r) n -> r q n", r=ROWS)[r].bitcast(I32),
                out_scale[r:P:QUAD, :].bitcast(I32),
            )
